import numpy as np, ml_dtypes
CORES = [3,11,19,27,35,43,51,59]
N = 8
import mx_ref
BF = ml_dtypes.bfloat16
def gentries(a):
    return np.ascontiguousarray(a.reshape(8, 16, -1).transpose(0, 2, 1)).reshape(8, -1)
def gtable(e):
    e = np.asarray(e); return np.ascontiguousarray(e.reshape(8, -1, 16).transpose(0, 2, 1)).reshape(128, -1).astype(np.int32)
def gcols(t, e):
    v = np.concatenate([t.reshape(8, 16, -1, 4), np.zeros((8, 16, 1, 4), BF)], axis=2)
    return np.ascontiguousarray(np.stack([v[g][:, e[g]] for g in range(8)])).reshape(128, -1)
def tile(rs):
    return np.stack(rs, axis=2).reshape(128, -1).astype(BF)
def pick(q, e):
    c = np.concatenate([q[0].reshape(128, -1, 4), np.zeros((128, 1, 4), np.uint8)], axis=1); s = np.concatenate([q[1], np.ones((16, 1), np.uint8)], axis=1)
    return (np.ascontiguousarray(c[:, e].reshape(128, -1)), np.ascontiguousarray(s[:, e]))
def join(*qs):
    return (np.concatenate([q[0] for q in qs], axis=1), np.concatenate([q[1] for q in qs], axis=1))
def put(q, e, v):
    c, s = q[0].reshape(128, -1, 4).copy(), q[1].copy(); c[:, e] = v[0].reshape(128, -1, 4); s[:, e] = v[1]
    return (c.reshape(128, -1), s)
def pk(c, s):
    return (np.ascontiguousarray(c), mx_ref.live(s))
def emit(q):
    return q[0], q[1]
def packed(v, rng):
    q = [mx_ref.quantize(np.ascontiguousarray(v[r])) for r in range(N)]
    return np.stack([a for a, b in q]), np.stack([mx_ref.plane(b, rng) for a, b in q])
def values_of_codes():
    e, c = np.zeros((128, 128, 4), np.float32), np.zeros((128, 2, 4), np.uint8)
    e[np.arange(128), np.arange(128), 0] = 1
    c[:127, :, 0] = np.arange(256).reshape(2, 128).T[:127]
    return mx_ref.matmul(mx_ref.quantize(e.reshape(128, 512).astype(BF)), (c.reshape(128, 8), np.full((16, 2), 127, np.uint8))).T.reshape(-1).astype(np.float64)
CODE_VALUE, SCALE_VALUE = values_of_codes(), 2.0 ** (np.arange(256) - 127.0)
def decode(q):
    return (CODE_VALUE[q[0]].reshape(16, 8, -1, 4) * SCALE_VALUE[q[1]][:, None, :, None] + 0.0).reshape(128, -1).astype(np.float32)
def f(rng, *shape):
    return mx_ref.flush((rng.standard_normal(shape, dtype=np.float32) * np.exp2(rng.integers(-2, 3, shape[:-1] + (1,)))).astype(BF))
def wide(rng, *shape, cols=0):
    v = rng.standard_normal(shape, dtype=np.float32) * np.exp2(rng.integers(-12, 13, shape)).astype(np.float32)
    if cols: v *= np.repeat(np.exp2(rng.integers(-cols, cols + 1, shape[:-2] + (1, shape[-1] // 4))) * (rng.random(shape[:-2] + (1, shape[-1] // 4)) > 0.0625), 4, axis=-1).astype(np.float32)
    return mx_ref.flush(v.astype(BF))
C, K, R, H = 256, 96, 3, 6
ROWS_USED = [(16 * g, 16 * g, 8) for g in range(8)] + [(16 * g + 1, 16 * g, 9) for g in range(8)] + [(8, 0, 10)]
def big(v):
    v = np.clip(v.astype(np.float32), -2.0 ** 21, 2.0 ** 21)
    v[np.abs(v) < np.float32(2.0 ** -16)] = 0
    return v.astype(BF)
def numbers_of(rng):
    return {"x": big(f(rng, N, 128, 4 * C)), "u": np.array(f(rng, N, 128, 512)), "v": np.array(f(rng, N, 128, 512))}
def links(rng):
    return np.stack([gtable(rng.integers(0, C, (8, C))) for r in range(N)])
def layers(rng):
    w = np.clip(big(f(rng, N, 128, 2048)).astype(np.float32) * np.float32(0.25), -1.0, 1.0)
    return w.astype(BF).reshape(N, 8, 16, 4, 8, 16, 4)
def weights(rng, w, still=[]):
    for i in still:
        w[:, :, i] = 0
        w[:, :, :, :, :, i] = 0
    c, p = packed(np.ascontiguousarray(w).reshape(N, 128, 2048), rng)
    return {"wc": c, "ws": p}
def setup_inputs(rng):
    return {**numbers_of(rng), "ol": links(rng), **weights(rng, layers(rng))}
def setup_inputs_ties(rng):
    d = numbers_of(rng)
    o = rng.permutation(N)
    x = d["x"].reshape(N, 8, 16, C, 4)
    x[:, :, :3] = 0
    x[:, :, :3, :, 0] = rng.integers(0, 3, (N, 8, 3, C)).astype(np.float32).astype(BF)
    k = np.ones(N, np.float32)
    k[o[0]] = 0
    k[o[1]] = -1
    u = d["u"].reshape(N, 128, 128, 4)
    for i, h, j in ROWS_USED:
        u[:, :, i] = 0
        u[:, h + j - 8, i, 0] = k.astype(BF)
    p = links(rng)
    e = np.stack([rng.permutation(C) for g in range(8)]).reshape(8, -1, 4)
    n = np.zeros((8, C), np.int64)
    np.put_along_axis(n, e.reshape(8, C), np.roll(e, -1, axis=2).reshape(8, C), axis=1)
    p[o[0]] = gtable(n)
    return {"x": x.reshape(N, 128, 4 * C), "u": u.reshape(N, 128, 512), "v": d["v"], "ol": p, **weights(rng, layers(rng), [0, 1, 2])}
def setup_inputs_near(rng):
    d = numbers_of(rng)
    o = rng.permutation(N) % 3
    x = d["x"].astype(np.float32).reshape(N, 8, 16, C, 4)
    x[:, :, 0] = 0
    x[:, :, 8:] = 0
    x[:, :, 0, :, 0] = rng.integers(0, 2, (N, 8, C)) * 2.0 - 1.0
    s = rng.integers(0, 16, (N, 8, 3, C))
    x[:, :, 8:11] = ((s[..., None] >> np.arange(4)) & 1) * np.exp2(np.arange(4) - 23.0)
    x[:, :, 11, :, 0] = 2.0 ** -10
    for r in range(N):
        for g in rng.permutation(8)[:4]: x[r, g, 0, rng.integers(C), 0] = 2.0 ** 20 * rng.choice([-1.0, 1.0])
    u = d["u"].reshape(N, 128, 128, 4)
    for i, h, j in ROWS_USED:
        u[:, :, i] = 0
        for r in range(N):
            k = 1.0 if o[r] == 0 else 2.0 ** -30
            u[r, h + j, i] = k
            if o[r] < 2:
                u[r, h, i, 0] = k
                u[r, h + 11, i, 0] = k
    return {"x": x.reshape(N, 128, 4 * C).astype(BF), "u": u.reshape(N, 128, 512), "v": d["v"], "ol": links(rng), **weights(rng, layers(rng), [0, 8, 9, 10, 11, 12, 13, 14, 15])}
def setup_inputs_chains(rng):
    d = numbers_of(rng)
    o = rng.permutation(N)
    p = []
    for r in range(N):
        e = np.zeros((8, C), np.int64)
        if o[r] == 0:
            n = rng.permutation(C)
            hub = np.sort(n[K - 1:])
            e[:, hub] = hub
            e[:, n[:K - 1]] = hub[rng.permutation(8 * (K - 1)) % (C - K + 1)].reshape(8, K - 1)
        elif o[r] % 2 == 0:
            for g in range(8):
                n = rng.permutation(C)
                e[g, n] = np.roll(n, -1)
        else:
            n = rng.permutation(C)
            low, hub, m = n[:K].reshape(-1, 8), n[K:], np.arange(K // 8)
            e[:, hub] = hub
            g = int(rng.integers(8))
            e[np.ix_([i for i in range(8) if i != g], n[:K])] = hub[rng.permutation(7 * K) % (C - K)].reshape(7, K)
            e[g, low[:, :7]] = low[:, 1:]
            e[g, low[:, 7]] = hub[:K // 8]
            e[g, hub[-(K // 8):]] = low[m, 7 - m % 8]
        p.append(gtable(e))
    x = d["x"].astype(np.float32).reshape(N, 8, 16, C, 4)
    k = rng.random((N, 1, 1, C, 1)) < 0.5
    k[:, :, :, 0] = True
    s = (1.125 + 0.25 * rng.integers(0, 4, x.shape)) * np.exp2(-rng.integers(8, 15, x.shape).astype(np.float64)) * rng.choice([-1.0, 1.0], x.shape)
    s[:, :, ::8, :, 0] = 1.96875 * rng.choice([-1.0, 1.0], (N, 8, 2, C))
    x = np.where(k, s, x).astype(np.float32).astype(BF)
    return {"x": x.reshape(N, 128, 4 * C), "u": d["u"], "v": d["v"], "ol": np.stack(p), **weights(rng, layers(rng))}
def setup_inputs_ends(rng):
    o = rng.permutation(N) % 4
    h = rng.permutation(8)
    a = np.full((N, 8, 16, C, 4), 2.0 ** 21)
    a[:, h[:4]] *= 1 - 0.1 * rng.random((N, 4, 16, C, 4))
    c = rng.integers(0, 2, (N, 1, 1, C, 1)) * 2.0 - 1.0
    c[o == 0] = 1
    c[o == 1] = -1
    a = a * c
    a[o == 3] = 2.0 ** -24
    u = np.full((N, 128, 128, 4), 2.0 ** 30)
    u[o == 3] = 2.0 ** -30
    for g in h[4:]: u[:, np.arange(128) // 16 != g, 16 * g:16 * g + 2] = 0
    k = rng.integers(0, 2, (N, 1, 128, 1)) * 2.0 - 1.0
    k[:, :, 1::16] = 1
    u = u * k + 0.0
    v = rng.choice([-1.0, 1.0], (N, 128, 512)) * np.where(o % 2 == 0, 2.0 ** 30, 2.0 ** -30)[:, None, None]
    w = np.ones((N, 128, 2048), np.float32)
    t = np.zeros((N, 8, C), np.int64)
    for r in range(N):
        if o[r] == 0: t[r] = C - 1
        if o[r] == 2:
            t[r] = np.arange(C)
            w[r] = rng.choice([-1.0, 1.0], (128, 2048))
        if o[r] == 3: t[r] = rng.integers(0, 2, (8, C)) * (C - 1)
    x, u, v = [b.astype(np.float32).astype(BF) for b in (a.reshape(N, 128, 4 * C), u.reshape(N, 128, 512), v)]
    return {"x": x, "u": u, "v": v, "ol": np.stack([gtable(t[r]) for r in range(N)]), **weights(rng, w.astype(BF))}
def setup_inputs_spread(rng):
    d = setup_inputs(rng)
    d["x"] = big(wide(rng, N, 128, 4 * C, cols=6))
    return d
def check_inputs(d):
    b = []
    for k, lo, hi in (("x", -24, 21), ("u", -30, 30), ("v", -30, 30)):
        a = np.abs(d[k].astype(np.float32))
        if not (np.isfinite(a).all() and ((a == 0) | (a >= 2.0 ** lo) & (a <= 2.0 ** hi)).all()): b.append("a value of " + k)
    if not ((d["ol"] >= 0) & (d["ol"] < C)).all(): b.append("an entry of ol")
    none, least, most = [emit(mx_ref.quantize(np.full((128, 16), k, np.float32).astype(BF)))[1][0, 0] for k in (0.0, 2.0 ** -30, 1.0)]
    for r in range(N):
        if ((d["wc"][r] == 0x7F) | (d["wc"][r] == 0xFF)).any(): b.append("wc: a code that is no number")
        s = mx_ref.live(d["ws"][r])
        if ((s != none) & ((s < least) | (s > most))).any(): b.append("ws: a scale out of range")
        elif not (np.abs(decode(pk(d["wc"][r], d["ws"][r]))) <= 1).all(): b.append("W: a number beyond 1")
    return b
def places(s):
    return np.argsort(np.argsort(s, axis=-1, kind="stable"), axis=-1, kind="stable")
def reference(x, u, v, ol, wc, ws):
    qu = [mx_ref.quantize(u[r]) for r in range(N)]
    lay = [pk(wc[r], ws[r]) for r in range(N)]
    now = [x[r] for r in range(N)]
    link = [gentries(ol[r]).astype(np.int64) for r in range(N)]
    for t in range(R):
        means, sent, given, freed, spliced = [], [], [], [], []
        for r in range(N):
            q = mx_ref.quantize(now[r])
            s = mx_ref.matmul(qu[r], q) + np.float32(0.0)
            own = decode(q)
            birth, snap = places(s[8]), places(s[::16])
            hops = [link[r]]
            for i in range(H - 1): hops.append(np.take_along_axis(link[r], hops[-1], axis=1))
            read = hops[-1]
            for p in hops[::-1]: read = np.where(birth[p] <= snap, p, read)
            z = ((own + gcols(own.astype(BF), read).astype(np.float32)) * np.float32(0.5)).astype(BF)
            e = np.argsort(-s[1::16], axis=1, kind="stable")[:, :K]
            count = np.bincount(read.reshape(-1), minlength=C)
            d = np.sort(np.argsort(count, kind="stable")[:K])
            gone = np.zeros(C, bool)
            gone[d] = True
            l = np.tile(np.arange(C), (8, 1))
            for p in hops[::-1]: l = np.where(gone[p], l, p)
            means.append(z)
            sent.append(mx_ref.quantize(gcols(z, e)))
            given.append(e)
            freed.append(d)
            spliced.append(l)
        for r in range(N):
            b4 = (r + N - 1) % N
            a = sent[b4]
            da = decode(a)
            m = tile([mx_ref.matmul(pick(lay[r], np.arange(128 * b, 128 * b + 128)), a) * np.float32(0.0078125) + da[:, b::4] for b in range(4)])
            z = means[r].reshape(128, C, 4).copy()
            z[:, freed[r]] = m.reshape(128, K, 4)
            now[r] = z.reshape(128, 4 * C)
            link[r] = spliced[r]
            link[r][:, freed[r]] = given[b4]
    y, lk = np.zeros((N, 128, C), np.float32), np.zeros((N, 8, C), np.float32)
    oc, osc = np.zeros((N, 128, 4 * C), np.uint8), np.zeros((N, 16, C), np.uint8)
    for r in range(N):
        q = mx_ref.quantize(now[r])
        y[r] = mx_ref.matmul(mx_ref.quantize(v[r]), q)
        lk[r] = link[r]
        oc[r], osc[r] = emit(q)
    return {"y": y, "lk": lk, "oc": oc, "osc": osc}

@@ -1,0 +1,541 @@
+import numpy as np
+from concourse.bass import DstId, RemoteDMATransfer
+from concourse.mybir import dt, AluOpType, AxisListType, ActivationFunctionType
+
+OP = AluOpType
+AF = ActivationFunctionType
+ROUNDS, KEEP = 3, 96
+F, B, I, U, X4, U8 = "float32", "bfloat16", "int32", "uint16", "float8_e4m3fn_x4", "uint8"
+
+SCRATCH = {}
+
+
+def _sb(dtype, **widths):
+    for name in widths:
+        SCRATCH[name] = ("sbuf", [128, widths[name]], dtype)
+
+
+def _q(**widths):
+    for name in widths:
+        SCRATCH["c" + name] = ("sbuf", [128, widths[name]], X4)
+        SCRATCH["s" + name] = ("sbuf", [128, widths[name]], U8)
+
+
+_sb(B, XT=1024, UT=512, VTL=512)
+_sb(I, OL=16, PC=1, PI=4, OI=72, RI=32, CI=24, LI=144)
+_q(W=512, U=128, UP=384, V=128, X=1024, L=320, P=384, E=384)
+_q(K=1024)
+_q(C=1664)
+_sb(B, TK=4096)
+_sb(F, IR=256, ID=256, TI=128, BK=512, PF=16, RQ=256, BS=256, BE=256, TR=128, CY=368, CB=368, CW=16, CX=16, CT=16)
+_sb(U, OU=72)
+_sb(B, ME=256, KP=256, ON=288, EX=256)
+_sb(F, MS=512, SWS=256, SG=256, SWE=256, EG=256, SB2=2, DL=4, TH0=128, TH1=128)
+_sb(B, BT=1024, CT2=8192, AJ=1024)
+_sb(F, VH=1792, VT=1792, T6=80, CM=96, XX=192, MN=80, T1=32)
+_sb(B, FT=1024, FU=1024, Z=1024, ET=512, RT=512)
+_sb(F, AR=32, RW=32, EC=256, EP=48, EF=256, PK=96)
+_sb(U, EP16=16, EO=32, LS=144, LL=144, R16=16, NI16=16, M16=16, J16=16, L16=16)
+_sb(B, RD=512, XR=512, RX=512)
+_sb(F, XE=256, ES=96, RS=256)
+_sb(F, CA=8, CJ=512, CF=16, QQ=176, W3=24)
+_sb(B, RP=256, TO=256, FB=128, EQM=256, CU=256, OV=256, Z2=256, GN=256)
+_sb(F, SC=16, GS=256, M1=256, Y0=256, NS=256, SM=160, YA=256, YB=256, YX=352, NR=256, LW=16, YO=256)
+for _i in range(8):
+    SCRATCH["P%d" % _i] = ("psum", [128, 512], F)
+PS = ["P%d" % i for i in range(8)]
+PLACE = {"B": ("C", 0)}
+TILE_N = (128, 128, 192, 256)
+for _i in range(4):
+    PLACE["X%d" % _i] = ("X", 256 * _i)
+    PLACE["KR%d" % _i] = ("K", 128 * _i)
+    PLACE["C%d" % _i] = ("C", 256 + sum(TILE_N[:_i]))
+    PLACE["D%d" % _i] = ("C", 960 + sum(TILE_N[:_i]))
+for _i in range(3):
+    PLACE["E%d" % _i] = ("E", 128 * _i)
+for _i, _k in enumerate(("KS", "KB", "KT", "KU")):
+    PLACE[_k] = ("K", 512 + 128 * _i)
+
+SEMAPHORES = ["sV", "sA", "sP", "sG", "dX", "dU", "dO", "dW", "dVV", "dPad", "dY", "dLk", "dOc", "ls",
+              "aC0", "aC1", "aC2", "aL0", "aL1", "aL2"]
+
+
+def rank_program(g, core, T, topo):
+    rank = T.rank_of(core)
+    if rank is None:
+        return
+    cores = T.cores
+    n_ranks = len(cores)
+    nxt, prv = cores[(rank + 1) % n_ranks], cores[(rank - 1) % n_ranks]
+    eng = {"V": g.vector, "A": g.scalar, "P": g.tensor, "G": g, "S": g.sync}
+    own = {"V": "sV", "A": "sA", "P": "sP", "G": "sG"}
+    cnt, known, lastw, readers = {}, {q: {} for q in eng}, {}, {}
+
+    def sync(q, toks):
+        for s, n, clk in sorted(toks, key=lambda t: -sum(t[2].values())):
+            if known[q].get(s, 0) < n:
+                eng[q].wait_ge(T.sem[s], n)
+                for k in clk:
+                    known[q][k] = max(known[q].get(k, 0), clk[k])
+                known[q][s] = max(known[q].get(s, 0), n)
+
+    def deps(q, r, w):
+        toks, me = [], own.get(q)
+        for k in r:
+            if k in lastw and not (q == "P" and lastw[k][0] == "sP"):
+                toks.append(lastw[k])
+            if k in PS:
+                toks += [t for s, t in readers.get(k, {}).items() if s != me]
+        for k in w:
+            if k in lastw and not (q == "P" and lastw[k][0] == "sP"):
+                toks.append(lastw[k])
+            toks += [t for s, t in readers.get(k, {}).items() if s != me]
+        sync(q, toks)
+        return toks
+
+    def done(tok, r, w):
+        for k in r:
+            readers.setdefault(k, {})[tok[0]] = tok
+        for k in w:
+            lastw[k] = tok
+            readers[k] = {}
+
+    def emit(q, r, w, fn):
+        deps(q, r, w)
+        s = own[q]
+        fn(eng[q]).then_inc(T.sem[s], 1)
+        cnt[s] = cnt.get(s, 0) + 1
+        clk = dict(known[q])
+        clk[s] = cnt[s]
+        done((s, cnt[s], clk), r, w)
+
+    def dma(q, s, r, w, pairs):
+        deps(q, r, w)
+        for o, i in pairs:
+            eng[q].dma_start(o, i).then_inc(T.sem[s], 16)
+            cnt[s] = cnt.get(s, 0) + 16
+        done((s, cnt[s], dict(known[q])), r, w)
+
+    def tt(r, w, out, a, b, op):
+        emit("V", r, w, lambda e: e.tensor_tensor(out, a, b, op))
+
+    def ts(r, w, out, a, s1, o1, s2=None, o2=None):
+        if o2 is None:
+            emit("V", r, w, lambda e: e.tensor_scalar(out, a, s1, None, o1))
+        else:
+            emit("V", r, w, lambda e: e.tensor_scalar(out, a, s1, s2, o1, o2))
+
+    def cp(r, w, out, a):
+        emit("V", r, w, lambda e: e.tensor_copy(out, a))
+
+    def scan(r, w, out, d0, d1, init=0.0, o0=OP.mult, o1=OP.add):
+        emit("V", r, w, lambda e: e.tensor_tensor_scan(out, d0, d1, init, o0, o1))
+
+    def turn(r, w, out, a):
+        emit("V", r, w, lambda e: e.transpose(out, a))
+
+    def fill(w, ap, x):
+        emit("V", [], w, lambda e: e.memset(ap, x))
+
+    def quant(r, name, c0, c1, tile):
+        k, o = PLACE.get(name, (name, 0))
+        emit("V", r, [name if c0 == 0 else name + "b"],
+             lambda e: e.quantize_mx(T["c" + k][:, o + c0:o + c1], T["s" + k][:, o + c0:o + c1], tile))
+
+    def act(r, w, out, a, fn=AF.Copy, bias=0.0, scale=1.0, acc=None):
+        if acc is None:
+            emit("A", r, w, lambda e: e.activation(out, a, fn, bias, scale))
+        else:
+            emit("A", r, w, lambda e: e.activation(out, a, fn, bias, scale, accum_out=acc))
+
+    def mm(r, bank, n, L, l0, R, r0, start=True, stop=True):
+        L, lo_ = PLACE.get(L, (L, 0))
+        R, ro_ = PLACE.get(R, (R, 0))
+        l0, r0 = l0 + lo_, r0 + ro_
+        emit("P", r, [bank], lambda e: e.matmul_mx(
+            T[bank][:, 0:n], T["c" + L][:, l0:l0 + 128], T["s" + L][:, l0:l0 + 128],
+            T["c" + R][:, r0:r0 + n], T["s" + R][:, r0:r0 + n], start, stop))
+
+    def iota(w, out, pattern, base, cm):
+        emit("G", [], w, lambda e: e.iota(out, pattern, base, cm, allow_small_or_imprecise_dtypes=True))
+
+    def iotai(w, out, pattern, base, cm):
+        emit("G", [], w, lambda e: e.iota(out, pattern, base, cm))
+
+    dma("S", "dX", [], ["XT"], [(T.XT[:], T.x[:])])
+    dma("A", "dU", [], ["UT"], [(T.UT[:], T.u[:])])
+    dma("S", "dO", [], ["OL"], [(T.OL[:], T.ol[:])])
+    dma("A", "dW", [], ["W"], [(T.cW[:].bitcast(dt.uint8), T.wc[:]), (T.sW[:], T.ws[:])])
+    dma("S", "dVV", [], ["VTL"], [(T.VTL[:], T.v[:])])
+
+    iotai(["PC"], T.PC[:], [[0, 1]], 0, 1)
+    iotai(["OI"], T.OI[:, 0:8], [[16, 8]], 0, 0)
+    iotai(["OI"], T.OI[:, 8:16], [[16, 8]], 1, 0)
+    iotai(["OI"], T.OI[:, 16:24], [[0, 8]], 8, 0)
+    iotai(["OI"], T.OI[:, 24:40], [[1, 16]], 0, 0)
+    iotai(["OI"], T.OI[:, 40:56], [[16, 16]], 15, 0)
+    iotai(["OI"], T.OI[:, 56:72], [[1, 8], [0, 2]], 0, 0)
+    iota(["IR"], T.IR[:], [[0, 16], [1, 16]], 0, 0)
+    iota(["TI"], T.TI[:], [[1, 128]], 0, -1)
+    iota(["ID"], T.ID[:], [[1, 256]], 0, 0)
+    iota(["BK"], T.BK[:], [[1, 8], [0, 64]], 0, 0)
+    iota(["CW"], T.CW[:], [[16, 16]], 0, 0)
+    iota(["CT0"], T.CT[:], [[32, 8], [0, 2]], 0, 0)
+    iota(["CY"], T.CY[:], [[1, 368]], -112, 0)
+    cp(["OI"], ["OU"], T.OU[:], T.OI[:])
+    ts(["PC"], ["PI"], T.PI[:, 0:1], T.PC[:], 15, OP.bitwise_and)
+    ts(["PC"], ["PI1"], T.PI[:, 1:2], T.PC[:], 4, OP.arith_shift_right)
+    ts(["PI1"], ["PI2"], T.PI[:, 2:3], T.PI[:, 1:2], 1, OP.bitwise_and)
+    cp(["PI"], ["q"], T.PF[:, 0:1], T.PI[:, 0:1])
+    cp(["PI1"], ["g"], T.PF[:, 1:2], T.PI[:, 1:2])
+    cp(["PI2"], ["m1"], T.PF[:, 2:3], T.PI[:, 2:3])
+    ts(["m1"], ["m0"], T.PF[:, 3:4], T.PF[:, 2:3], -1.0, OP.mult, 1.0, OP.add)
+    ts(["q"], ["qn"], T.PF[:, 4:5], T.PF[:, 0:1], -1.0, OP.mult, -0.5, OP.add)
+    ts(["IR", "q"], ["RQ"], T.RQ[:], T.IR[:], T.PF[:, 0:1], OP.subtract)
+    ts(["RQ"], ["ME"], T.ME[:], T.RQ[:], 0.0, OP.is_equal)
+    ts(["IR"], ["KP"], T.KP[:], T.IR[:], 0.5, OP.is_gt)
+    ts(["RQ"], ["BE"], T.BE[:], T.RQ[:], 0.0, OP.is_gt, 512.0, OP.mult)
+    ts(["ME"], ["EX"], T.EX[:], T.ME[:], -2.0 ** 20, OP.mult)
+    tt(["BE", "EX"], ["EX"], T.EX[:], T.BE[:], T.EX[:], OP.add)
+    ts(["q"], ["xq"], T.PF[:, 5:6], T.PF[:, 0:1], -512.0, OP.mult, 7680.0, OP.add)
+    for i in range(4):
+        ts(["xq"], ["xq4"], T.PF[:, 8 + i:9 + i], T.PF[:, 5:6], -4.0, OP.mult, float(i), OP.add)
+    quant(["UT"], "U", 0, 128, T.UT[:, 0:512])
+    emit("V", ["U", "OU"], ["UPc"], lambda e: e.tensor_copy(
+        T.cUP[:, 0:384].bitcast(dt.uint32), T.cU[:, 0:128].bitcast(dt.uint32).indirect(T.OU[:, 0:24])))
+    emit("V", ["U", "OU"], ["UPs"], lambda e: e.tensor_copy(T.sUP[:, 0:384], T.sU[:, 0:128].indirect(T.OU[:, 0:24])))
+    UPK = ["UPc", "UPs"]
+    quant(["XT"], "X0", 0, 256, T.XT[:])
+    ts(["RQ"], ["BS"], T.BS[:], T.RQ[:], 0.0, OP.is_ge, -2.0 ** 90, OP.mult)
+    ts(["RQ"], ["BE"], T.BE[:], T.RQ[:], 0.0, OP.is_ge, 2.0 ** 90, OP.mult)
+    ts(["TI"], ["TR"], T.TR[:], T.TI[:], 0.0, OP.is_le)
+    fill(["TK"], T.TK[:], 0.0)
+    for a in range(4):
+        fill(["CT2"], T.CT2[:, 1024 * a:1024 * a + 4 * TILE_N[a]], 0.0)
+        act(["CT2"], ["CT3"], T.CT2[:, 4096 + 1024 * a:4096 + 1024 * a + 4 * TILE_N[a]],
+            T.CT2[:, 1024 * a:1024 * a + 4 * TILE_N[a]])
+    fill(["AR"], T.AR[:], 0.0)
+    dma("S", "dPad", ["X0"], ["pad"], [(T.cL[:, 288:320].bitcast(dt.uint8), T.cX[:, 0:32].bitcast(dt.uint8)),
+                                       (T.sL[:, 288:320], T.sX[:, 0:32])])
+
+    def late_constants():
+        for b in range(4):
+            o = 512 * b
+            ts(["TI", "TK"], ["TK%d" % b], T.TK[:, o + b:o + 512:4], T.TI[:], 0.0, OP.is_equal, 128.0, OP.mult)
+        for b in range(4):
+            quant(["TK%d" % b], "KR%d" % b, 0, 128, T.TK[:, 512 * b:512 * b + 512])
+
+    def birth_constants():
+        ts(["BK", "g"], ["TKS"], T.TK[:, 2048:2560], T.BK[:], T.PF[:, 1:2], OP.is_equal)
+        for i in range(2):
+            ts(["TI", "TK"], ["TKB"], T.TK[:, 2560 + i:3072:4], T.TI[:], 0.0, OP.mult, 256.0, OP.add)
+            o = 3072 + 512 * i
+            ts(["BK", "g", "TK"], ["TKT"], T.TK[:, o + 2 + i:o + 512:4], T.BK[:, 2:512:4], T.PF[:, 1:2], OP.is_equal)
+        for i, k in enumerate(("KS", "KB", "KT", "KU")):
+            quant(["TKS", "TKB", "TKT", "TK"], k, 0, 128, T.TK[:, 2048 + 512 * i:2560 + 512 * i])
+        ts(["CW", "xq"], ["CX"], T.CX[:], T.CW[:], T.PF[:, 5:6], OP.subtract)
+        ts(["PC"], ["PI3"], T.PI[:, 3:4], T.PC[:], 31, OP.bitwise_and)
+        cp(["PI3"], ["x32"], T.PF[:, 6:7], T.PI[:, 3:4])
+        ts(["x32", "xq"], ["x32q"], T.PF[:, 7:8], T.PF[:, 6:7], T.PF[:, 5:6], OP.add)
+        ts(["CT0", "x32q"], ["CT"], T.CT[:], T.CT[:], T.PF[:, 7:8], OP.add)
+
+    def count_constants():
+        ts(["CY", "q"], ["CY"], T.CY[:], T.CY[:], T.PF[:, 0:1], OP.subtract)
+        ts(["CY"], ["CB"], T.CB[:], T.CY[:], 128.0, OP.is_equal, 512.0, OP.mult)
+        ts(["CY"], ["CY"], T.CY[:], T.CY[:], 0.0, OP.is_equal)
+        tt(["CY", "CB"], ["CB"], T.CB[:], T.CB[:], T.CY[:], OP.add)
+        fill(["ON"], T.ON[:, 0:32], 1.0)
+        fill(["ZR"], T.ON[:, 32:288], 0.0)
+        fill(["CM6"], T.CM[:], 0.0)
+        fill(["Q4z"], T.QQ[:, 48:80], 0.0)
+        fill(["ETz"], T.ET[:], 0.0)
+        fill(["RTz"], T.RT[:], 0.0)
+        quant(["VTL"], "V", 0, 128, T.VTL[:])
+
+    ts(["CW", "q"], ["CW"], T.CW[:], T.CW[:], T.PF[:, 0:1], OP.add)
+    cp(["OL"], ["LW"], T.LW[:], T.OL[:])
+    cp(["OL"], ["L16"], T.L16[:], T.OL[:])
+
+    BC, BC15, BC32 = T.OU[:, 24:40], T.OU[:, 40:56], T.OU[:, 56:72]
+    E15 = slice(15, 256, 16)
+    rid, pid = topo.addr(nxt)[0], topo.addr(nxt)[1]
+    mask = topo.mask(core, nxt)
+    n_eng = len(topo.engines(core, nxt))
+    n_arr = len(topo.engines(prv, core))
+    sent = [0]
+
+    def send(r, out, src, rsem):
+        deps("G", r, [])
+        g.remote_dma(out, src, T.sem[rsem], T.sem.ls, pid, rid, mask)
+        sent[0] += n_eng
+
+    pending = []
+
+    for t in range(ROUNDS):
+        X = "X%d" % t
+        XK = [X, X + "s"]
+        mm(XK + UPK, "P7", 256, "UP", 0, X, 0)
+        mm(XK + UPK, "P5", 128, X, 0, "UP", 256)
+        mm(XK + UPK, "P6", 128, X, 128, "UP", 256)
+        mm(XK + UPK, "P4", 256, "UP", 256, X, 0)
+        mm(XK + UPK, "P3", 256, "UP", 128, X, 0)
+        act(["P5"], ["SB0"], T.SB2[:, 0:1], T.P5[:, 0:1])
+        act(["P6"], ["SB1"], T.SB2[:, 1:2], T.P6[:, 0:1])
+        act(["SB0", "SB1"], ["DL"], T.DL[:, 0:2], T.SB2[:, 0:2], AF.Abs, 0.0, 1.25 * 2.0 ** -24)
+        tt(["P7", "ME"], ["MS"], T.MS[:, 0:256], T.P7[:, 0:256], T.ME[:], OP.mult)
+        if t == 0:
+            birth_constants()
+        ts(["DL"], ["DL2"], T.DL[:, 2:4], T.DL[:, 0:2], 2.0 ** -120, OP.add)
+        for h in range(2):
+            act(["TR", "DL2", "SB0", "SB1"], ["TH%d" % h], T["TH%d" % h][:], T.TR[:], AF.Identity,
+                T.SB2[:, h:h + 1], T.DL[:, 2 + h:3 + h])
+        for f in pending[:2]:
+            f()
+        scan(["KP", "MS"], ["SWS"], T.SWS[:], T.KP[:], T.MS[:, 0:256])
+        tt(["P7", "BS"], ["SG"], T.SG[:], T.P7[:, 0:256], T.BS[:], OP.add)
+        ts(["P4", "SB0"], ["BTa"], T.BT[:, 512:1024:4], T.P4[:, 128:256], T.SB2[:, 0:1], OP.is_ge)
+        ts(["P4", "SB1"], ["BTb"], T.BT[:, 1:512:4], T.P4[:, 0:128], T.SB2[:, 1:2], OP.is_gt)
+        tt(["P3", "ME"], ["MSE"], T.MS[:, 256:512], T.P3[:, 0:256], T.ME[:], OP.mult)
+        tt(["SWS", "SG", "OU"], ["BTe"], T.BT[:, 2:1024:4], T.SWS[:].indirect(BC15), T.SG[:], OP.is_lt)
+        scan(["KP", "MSE"], ["SWE"], T.SWE[:], T.KP[:], T.MS[:, 256:512])
+        tt(["P3", "BE"], ["EG"], T.EG[:], T.P3[:, 0:256], T.BE[:], OP.add)
+        tt(["P4", "TH0"], ["BTc"], T.BT[:, 0:512:4], T.P4[:, 0:128], T.TH0[:], OP.is_ge)
+        tt(["P4", "TH1"], ["BTd"], T.BT[:, 513:1024:4], T.P4[:, 128:256], T.TH1[:], OP.is_ge)
+
+        tt(["SWE", "EG", "OU"], ["BTf"], T.BT[:, 3:1024:4], T.SWE[:].indirect(BC15), T.EG[:], OP.is_gt)
+
+        def pair(s, m):
+            bank, w, k, op = (("P7", T.SWS, "SWS", OP.is_gt), ("P3", T.SWE, "SWE", OP.is_lt))[s]
+            if m:
+                o, n = 4096 * s + 1024 * (m // 4), 64 * m
+                v = T.CT2[:, o + m % 4:o + n:4]
+                ts([bank, k, "CT2", "CT3"], ["ct%d.%d" % (s, m)], v, T[bank][:, 0:16 * m], w[:, 16 * m + 15:16 * m + 16], op)
+                j = m % 4
+                act(["ct%d.%d" % (s, m), "AR"], ["AR%d.%d" % (s, m), "AJ%d" % j], T.AJ[:, 256 * j:256 * j + 16 * m], v,
+                    AF.Copy, 0.0, 1.0, T.AR[:, 16 * s + m:16 * s + m + 1])
+
+        def pair_sum(s, a):
+            o, n, k, bank = 4096 * s + 1024 * a, TILE_N[a], "CD"[s] + str(a), ("P4", "P5")[s]
+            quant(["ct%d.%d" % (s, m) for m in range(4 * a, 4 * a + 4) if m] + ["CT2", "CT3"], k, 0, n, T.CT2[:, o:o + 4 * n])
+            mm([k, "KS"], bank, n, "KS", 0, k, 0, False, a == 3)
+
+        def row_sum(s):
+            scan(["KP", ("BTe", "BTf")[s]], ["RD%d" % s], T.RD[:, 256 * s:256 * s + 256], T.KP[:], T.BT[:, 2 + s:1024:4])
+            tt(["RD%d" % s, "AR"] + ["AR%d.%d" % (s, m) for m in range(1, 16)], ["RW%d" % s], T.RW[:, 16 * s:16 * s + 16],
+               T.RD[:, 256 * s + 15:256 * s + 256:16], T.AR[:, 16 * s:16 * s + 16], OP.add)
+
+        pair(0, 15)
+        quant(["BTa", "BTb", "BTc", "BTd", "BTe", "BTf"], "B", 0, 256, T.BT[:])
+        mm(["B", "KB"], "P6", 256, "KB", 0, "B", 0)
+        mm(["B", "KT"], "P4", 256, "KT", 0, "B", 0, True, False)
+        if t == 0:
+            late_constants()
+        for b in range(4):
+            mm(XK + ["KR%d" % b], ("P0", "P1", "P2", "P5")[b], 256, "KR%d" % b, 0, X, 0)
+        for b in range(4):
+            k = ("P0", "P1", "P2", "P5")[b]
+            act([k], ["FT%d" % b], T.FT[:, 256 * b:256 * b + 256], T[k][:, 0:256], AF.Copy, 0.0, 2.0 ** -8)
+        mm(["B", "KU"], "P5", 256, "KU", 0, "B", 0, True, False)
+        pair(0, 14)
+        tt(["P6", "ID"], ["V0"], T.VH[:, 1536:1792], T.P6[:, 0:256], T.ID[:], OP.add)
+        pair(0, 13)
+        pair(0, 12)
+        for m in range(11, 3, -1):
+            pair(0, m)
+        for f in pending[2:]:
+            f()
+        for m in range(3, 0, -1):
+            pair(0, m)
+        for a in range(4):
+            pair_sum(0, a)
+        if t == 0:
+            count_constants()
+        for i in range(6):
+            src, k = (T.VH[:, 1536:1792], "V0") if i == 0 else (T.VH[:, 256 * i - 256:256 * i], "VH%d" % (i - 1))
+            act([k, "L16"], ["VH%d" % i], T.VH[:, 256 * i:256 * i + 256], src.indirect(T.L16[:]),
+                AF.Identity, 65536.0)
+            if i == 0:
+                row_sum(0)
+                act(["RW0", "OU"], ["XR"], T.XR[:, 0:256], T.RW[:, 0:16].indirect(BC))
+        for m in range(15, 7, -1):
+            pair(1, m)
+        turn(["XR"], ["XS"], T.XR[:, 256:512], T.XR[:, 0:256])
+        turn(["P4"], ["TT"], T.VT[:, 1536:1792], T.P4[:, 0:256])
+        scan(["EX", "XS"], ["XE"], T.XE[:], T.EX[:], T.XR[:, 256:512], 0.0, OP.add, OP.max)
+        for m in range(7, 0, -1):
+            pair(1, m)
+            if m == 6:
+                tt(["TT", "CT"], ["T1a"], T.T1[:, 0:16], T.VT[:, 1536:1792:16], T.CT[:], OP.add)
+            if m == 4:
+                tt(["T1a", "XE"], ["T1b"], T.T1[:, 16:32], T.T1[:, 0:16], T.XE[:, E15], OP.subtract)
+        for i in range(5):
+            act(["T1b"], ["T6%d" % i], T.T6[:, 16 * i:16 * i + 16], T.T1[:, 16:32], AF.Identity, 255.5 + 65536.0 * (i + 1), 256.0)
+        act(["FT0", "FT1", "FT2", "FT3"], ["FU"], T.FU[:], T.FT[:])
+        for a in range(4):
+            pair_sum(1, a)
+        row_sum(1)
+        for i in range(6):
+            turn(["VH%d" % i], ["VT%d" % i], T.VT[:, 256 * i:256 * i + 256], T.VH[:, 256 * i:256 * i + 256])
+        scan(["EX", "P5"], ["EC"], T.EC[:], T.EX[:], T.P5[:, 0:256], 0.0, OP.add, OP.max)
+        VTK = ["VT%d" % i for i in range(6)]
+        tt(VTK[:5] + ["T6%d" % i for i in range(5)] + ["CM6"], ["CM"], T.CM[:, 0:80], T.VT[:, 0:1280:16], T.T6[:], OP.is_gt)
+        tt(["CX", "RW1"], ["EPa"], T.EP[:, 0:16], T.CX[:], T.RW[:, 16:32], OP.subtract)
+        ts(["CM", "CM6"], ["XXa"], T.XX[:, 0:96], T.CM[:], 2.0 ** 20, OP.mult)
+        tt(["EPa", "EC"], ["EP"], T.EP[:, 16:32], T.EP[:, 0:16], T.EC[:, E15], OP.add)
+        tt(["XXa"] + VTK, ["XXb"], T.XX[:, 96:192], T.XX[:, 0:96], T.VT[:, 0:1536:16], OP.add)
+        cp(["EP"], ["EP16"], T.EP16[:], T.EP[:, 16:32])
+        tt(["XXb"], ["MNa"], T.MN[:, 0:48], T.XX[:, 96:144], T.XX[:, 144:192], OP.min)
+        tt(["MNa"], ["MNb"], T.MN[:, 48:64], T.MN[:, 0:16], T.MN[:, 16:32], OP.min)
+        tt(["MNa", "MNb"], ["RI0"], T.RI[:, 0:16], T.MN[:, 48:64], T.MN[:, 32:48], OP.min)
+        ts(["RI0"], ["RI1"], T.RI[:, 16:32], T.RI[:, 0:16], 255, OP.bitwise_and)
+        cp(["RI1"], ["RI2"], T.EP[:, 32:48], T.RI[:, 16:32])
+        act(["RI2", "OU"], ["RX"], T.RX[:, 0:256], T.EP[:, 32:48].indirect(BC))
+        cp(["ID", "EP16"], ["EF"], T.EF[:, 0:256].indirect(T.EP16[:]), T.ID[:])
+        turn(["RX"], ["RY"], T.RX[:, 256:512], T.RX[:, 0:256])
+        scan(["EX", "RY"], ["RS"], T.RS[:], T.EX[:], T.RX[:, 256:512], 0.0, OP.add, OP.max)
+        ts(["RS", "xq"], ["R16"], T.R16[:], T.RS[:, E15], T.PF[:, 5:6], OP.subtract)
+        for z in range(8):
+            act(["CB", "R16"], ["CJ%d" % (z % 2), "CA%d" % z], T.CJ[:, 256 * (z % 2):256 * (z % 2) + 256], T.CB[:, 112 - 16 * z:368 - 16 * z].indirect(T.R16[:]),
+                AF.Copy, 0.0, 1.0, T.CA[:, z:z + 1])
+        for b in range(4):
+            f = T.FT[:, 256 * b:256 * b + 256]
+            tt(["FT%d" % b, "FU", "R16"], ["Z%d" % b], T.Z[:, b:1024:4], f.indirect(T.R16[:]),
+               T.FU[:, 256 * b:256 * b + 256], OP.add)
+            if b == 1:
+                scan(["EX", "EF"], ["ES"], T.ES[:], T.EX[:, 0:96], T.EF[:, 0:96], 0.0, OP.add, OP.max)
+            if b == 2:
+                for i in range(4):
+                    ts(["ES", "xq4"], ["EO%d" % i], T.EO[:, 8 * i:8 * i + 6], T.ES[:, 15:96:16], 4.0, OP.mult,
+                       T.PF[:, 8 + i:9 + i], OP.add)
+        ZK = ["Z0", "Z1", "Z2", "Z3"]
+        for b in range(4):
+            act(ZK + ["EO%d" % b], ["ET%d" % b], T.ET[:, b:384:4], T.Z[:].indirect(T.EO[:, 8 * b:8 * b + 6]))
+        act(["EF"], ["PKa"], T.PK[:, 0:48], T.EF[:, 48:96], AF.Copy, 0.0, 256.0)
+        lo = KEEP * (ROUNDS - 1 - t)
+
+        def send_columns():
+            quant(["ET0", "ET1", "ET2", "ET3", "ETz"], "E%d" % t, 0, 128, T.ET[:])
+            send(["E%d" % t], T.cL[:, lo:lo + KEEP].bitcast(dt.uint8),
+                 T.cE[:, 128 * t:128 * t + KEEP].bitcast(dt.uint8), "aC%d" % t)
+            send(["E%d" % t], T.sL[:, lo:lo + KEEP], T.sE[:, 128 * t:128 * t + KEEP], "aC%d" % t)
+            send(["LS%d" % t], T.LL[:, 48 * t:48 * t + 48], T.LS[:, 48 * t:48 * t + 48], "aL%d" % t)
+            lastw["L%d" % t] = ("aC%d" % t, 2 * n_arr, {})
+            lastw["LL%d" % t] = ("aL%d" % t, n_arr, {})
+        tt(["PKa", "EF"], ["PKb"], T.PK[:, 48:96], T.PK[:, 0:48], T.EF[:, 0:48], OP.add)
+        quant(ZK, "P", 0, 256, T.Z[:])
+        cp(["PKb"], ["LS%d" % t], T.LS[:, 48 * t:48 * t + 48], T.PK[:, 48:96])
+        cp(["CA%d" % z for z in range(8)], ["CI0"], T.CI[:, 0:8], T.CA[:])
+        ts(["CI0"], ["CI1"], T.CI[:, 8:16], T.CI[:, 0:8], 511, OP.bitwise_and)
+        ts(["CI0"], ["CI2"], T.CI[:, 16:24], T.CI[:, 0:8], 9, OP.arith_shift_right)
+        ts(["CI1", "CI2"], ["CF"], T.CF[:], T.CI[:, 8:24], 16.0, OP.min)
+        Q1, Q2, Q3, Q4, Q5, Q6, Q7 = [(a, a + 32) for a in (0, 16, 32, 48, 80, 112, 144)]
+
+        def qq(q, a=0, b=32, step=1, p=0, np_=128):
+            return T.QQ[p:p + np_, q[0] + a:q[0] + b:step]
+        cp(["CF"], ["Q1"], qq(Q1, 0, 16, 1, 0, 64), T.CF[64:128, :])
+        cp(["CF"], ["Q1b"], qq(Q1, 0, 16, 1, 64, 64), T.CF[0:64, :])
+        tt(["CF", "Q1", "Q1b"], ["Q2"], qq(Q2, 0, 16), T.CF[:], qq(Q1, 0, 16), OP.add)
+        for a in range(4):
+            b = a ^ 1
+            cp(["Q2"], ["Q3%d" % a], qq(Q3, 0, 16, 1, 32 * a, 32), qq(Q2, 0, 16, 1, 32 * b, 32))
+        tt(["Q2", "Q30", "Q31", "Q32", "Q33", "Q4z"], ["Q4"], qq(Q4, 0, 16), qq(Q2, 0, 16), qq(Q3, 0, 16), OP.add)
+        turn(["Q4", "Q4z"], ["Q5"], qq(Q5), qq(Q4))
+        tt(["Q5"], ["Q6"], qq(Q6, 0, 16), qq(Q5, 0, 16), qq(Q5, 16, 32), OP.add)
+        tt(["Q5"], ["Q6b"], qq(Q6, 16, 32), qq(Q5, 0, 16), qq(Q5, 16, 32), OP.add)
+        turn(["Q6", "Q6b"], ["Q7"], qq(Q7), qq(Q6))
+        ts(["Q7", "m0"], ["W3a"], T.W3[:, 0:8], qq(Q7, 0, 16, 2), T.PF[:, 3:4], OP.mult)
+        act(["Q7", "m1"], ["W3b"], T.W3[:, 8:16], qq(Q7, 1, 16, 2), AF.Copy, 0.0, T.PF[:, 2:3])
+        send_columns()
+        tt(["W3a", "W3b"], ["W3"], T.W3[:, 16:24], T.W3[:, 0:8], T.W3[:, 8:16], OP.add)
+        act(["W3", "OU"], ["RP"], T.RP[:], T.W3[:, 16:24].indirect(BC32))
+        turn(["RP"], ["TO"], T.TO[:], T.RP[:])
+        act(["TO", "qn"], ["AJ0", "AC"], T.AJ[:, 0:256], T.TO[:], AF.Sign, T.PF[:, 4:5], 1.0, T.SC[:, 0:1])
+        ts(["AC"], ["F1"], T.SC[:, 2:3], T.SC[:, 0:1], 64.0, OP.is_le)
+        ts(["AC"], ["N1"], T.SC[:, 1:2], T.SC[:, 0:1], -0.5, OP.mult, 128.0, OP.add)
+        ts(["ON", "F1"], ["FB"], T.FB[:, 0:32], T.ON[:, 0:32], T.SC[:, 2:3], OP.mult)
+        ts(["AC", "N1"], ["NF"], T.SC[:, 3:4], T.SC[:, 0:1], 64.0, OP.is_gt, T.SC[:, 1:2], OP.mult)
+        ts(["ON", "NF"], ["FBb"], T.FB[:, 32:64], T.ON[:, 0:32], T.SC[:, 3:4], OP.mult)
+        turn(["FB", "FBb"], ["FX"], T.FB[:, 64:128], T.FB[:, 0:64])
+        emit("V", ["FX"], ["SF"], lambda e: e.tensor_reduce(T.SC[:, 4:5], T.FB[:, 64:80], AxisListType.X, OP.add))
+        emit("V", ["FX"], ["NP"], lambda e: e.tensor_reduce(T.SC[:, 5:6], T.FB[:, 96:112], AxisListType.X, OP.max))
+        ts(["SF"], ["TS"], T.SC[:, 6:7], T.SC[:, 4:5], -1.0, OP.mult, 16.0, OP.add)
+        ts(["NP"], ["ND"], T.SC[:, 7:8], T.SC[:, 5:6], -1.0, OP.mult, float(KEEP), OP.add)
+        ts(["TO", "TS"], ["EQM"], T.EQM[:], T.TO[:], T.SC[:, 6:7], OP.is_equal)
+        scan(["EQM", "ZR"], ["CU"], T.CU[:], T.EQM[:], T.ON[:, 32:288], 0.0, OP.add, OP.max)
+        ts(["CU", "ND"], ["OV"], T.OV[:], T.CU[:], T.SC[:, 7:8], OP.is_gt)
+        tt(["TO", "OV"], ["Z2x"], T.Z2[:], T.TO[:], T.OV[:], OP.add)
+        ts(["Z2x", "TS"], ["GN"], T.GN[:], T.Z2[:], T.SC[:, 6:7], OP.is_le)
+        scan(["GN", "ZR"], ["GS"], T.GS[:], T.GN[:], T.ON[:, 32:288], 255.0, OP.add, OP.max)
+        tt(["GS", "GN"], ["M1"], T.M1[:], T.GS[:], T.GN[:], OP.mult)
+        tt(["M1", "ID"], ["Y0"], T.Y0[:], T.M1[:], T.ID[:], OP.max)
+        scan(["EX", "Y0"], ["NSx"], T.NS[:], T.EX[:], T.Y0[:], 0.0, OP.add, OP.max)
+        ts(["NSx", "xq"], ["NI16"], T.NI16[:], T.NS[:, E15], T.PF[:, 5:6], OP.subtract)
+        ts(["NSx", "xq"], ["NS"], T.SM[:, 128:144], T.NS[:, E15], T.PF[:, 5:6], OP.subtract)
+        for b in range(4):
+            k = PS[b]
+            mm(["L%d" % t, "pad", "W"], k, 128, "W", 128 * b, "L", lo, True, False)
+            mm(["L%d" % t, "pad", "KR%d" % b], k, 128, "KR%d" % b, 0, "L", lo, False, True)
+        for b in range(2):
+            act([PS[b], "RTz"], ["RT%d" % b], T.RT[:, b:384:4], T[PS[b]][:, 0:96], AF.Copy, 0.0, 2.0 ** -7)
+        for b in range(2, 4):
+            ts([PS[b], "RTz"], ["RT%d" % b], T.RT[:, b:384:4], T[PS[b]][:, 0:96], 2.0 ** -7, OP.mult)
+        quant(["RT0", "RT1", "RT2", "RT3", "RTz"], "P", 256, 384, T.RT[:])
+        XN = "X%d" % (t + 1)
+        emit("V", ["P", "Pb", "NI16"], [XN], lambda e: e.tensor_copy(
+            T.cX[:, 256 * t + 256:256 * t + 512].bitcast(dt.uint32), T.cP[:, :].bitcast(dt.uint32).indirect(T.NI16[:])))
+        emit("A", ["P", "Pb", "NI16"], [XN + "s"], lambda e: e.activation(
+            T.sX[:, 256 * t + 256:256 * t + 512], T.sP[:, :].indirect(T.NI16[:]), AF.Copy))
+        res = T.SM[:, 128:144]
+        sm = [T.SM[:, 16 * i:16 * i + 16] for i in range(8)]
+        ts(["NS"], ["GW"], sm[0], res, 256.0, OP.is_ge)
+        tt(["LW", "CW"], ["D1"], sm[1], T.LW[:], T.CW[:], OP.subtract)
+        tt(["NS", "LW"], ["E1x"], sm[2], res, T.LW[:], OP.subtract)
+        tt(["GW", "D1"], ["D2"], sm[3], sm[0], sm[1], OP.mult)
+        tt(["GW", "E1x"], ["E2x"], sm[4], sm[0], sm[2], OP.mult)
+        tt(["D2", "CW"], ["D3"], sm[5], sm[3], T.CW[:], OP.add)
+        tt(["E2x", "LW"], ["E3"], sm[6], sm[4], T.LW[:], OP.add)
+        cp(["D3"], ["M16"], T.M16[:], sm[5])
+        cp(["E3"], ["J16"], T.J16[:], sm[6])
+
+        def chain(t=t):
+            src, k = T.Y0, "Y0"
+            for i in range(5):
+                dst, kd = ((T.YA, "YA"), (T.YB, "YB"))[i % 2] if i < 4 else (T.YX, "YX")
+                act([k, "M16"], [kd], dst[:, 0:256], src[:, 0:256].indirect(T.M16[:]))
+                src, k = dst, kd
+            act(["YX", "YXe", "J16"], ["M1"], T.M1[:], T.YX[:].indirect(T.J16[:]))
+
+        def unpack(t=t):
+            LL = "LL%d" % t
+            cp([LL], ["LI0"], T.LI[:, 0:48], T.LL[:, 48 * t:48 * t + 48])
+            ts(["LI0"], ["LI1"], T.LI[:, 48:96], T.LI[:, 0:48], 255, OP.bitwise_and)
+            ts(["LI0"], ["LI2"], T.LI[:, 96:144], T.LI[:, 0:48], 8, OP.arith_shift_right)
+            cp(["LI1", "LI2"], ["YXe"], T.YX[:, 256:352], T.LI[:, 48:144])
+
+        def relink():
+            scan(["EX", "M1"], ["NRx"], T.NR[:], T.EX[:], T.M1[:], 0.0, OP.add, OP.max)
+            r = T.SM[:, 144:160]
+            ts(["NRx", "xq"], ["NR"], r, T.NR[:, E15], T.PF[:, 5:6], OP.subtract)
+            ts(["NR"], ["FL"], sm[0], r, 256.0, OP.is_ge)
+            tt(["CW", "NR"], ["G1"], sm[1], T.CW[:], r, OP.subtract)
+            tt(["FL", "G1"], ["G2"], sm[2], sm[0], sm[1], OP.mult)
+            tt(["G2", "NR"], ["LW"], T.LW[:], sm[2], r, OP.add)
+            cp(["LW"], ["L16"], T.L16[:], T.LW[:])
+        pending = [unpack, chain, relink]
+
+    mm(["V", "X3", "X3s"], "P7", 256, "V", 0, "X3", 0)
+    dma("S", "dOc", ["X3", "X3s"], ["oc"], [(T.oc[:, :], T.cX[:, 768:1024].bitcast(dt.uint8))] + [
+        (T.osc[4 * k:4 * k + 4, :], T.sX[32 * k:32 * k + 4, 768:1024]) for k in range(4)])
+    pending[0]()
+    pending[1]()
+    cp(["P7"], ["YO"], T.YO[:], T.P7[:, 0:256])
+    dma("S", "dY", ["YO"], ["y"], [(T.y[:, :], T.YO[:])])
+    ts(["M1"], ["GS"], T.GS[:], T.M1[:], 256.0, OP.is_ge)
+    tt(["ID", "M1"], ["NRx"], T.NR[:], T.ID[:], T.M1[:], OP.subtract)
+    tt(["GS", "NRx"], ["Y0"], T.Y0[:], T.GS[:], T.NR[:], OP.mult)
+    tt(["Y0", "M1"], ["NSx", "NS"], T.NS[:], T.Y0[:], T.M1[:], OP.add)
+    dma("S", "dLk", ["NS"], ["lk"], [(T.lk[:, :], T.NS[0:128:16, :])])
+    for s in cnt:
+        if known["S"].get(s, 0) < cnt[s]:
+            g.sync.wait_ge(T.sem[s], cnt[s])
+    g.wait_ge(T.sem.ls, sent[0])

@@ -26,7 +26,7 @@ _sb(I, OL=16, PC=1, PI=4, OI=72, RI=32, CI=24, LI=144)
 _q(W=512, U=128, UP=384, V=128, X=1024, L=320, P=384, E=384)
 _q(K=1024)
 _q(C=1664)
-_sb(B, TK=4096)
+_sb(B, TK=5120)
 _sb(F, IR=256, ID=256, TI=128, BK=512, PF=16, RQ=256, BS=256, BE=256, TR=128, CY=368, CB=368, CW=16, CX=16, CT=16)
 _sb(U, OU=72)
 _sb(B, ME=256, KP=256, ON=288, EX=256)
@@ -35,12 +35,12 @@ _sb(B, BT=1024, CT2=8192, AJ=1024)
 _sb(F, VH=1792, VT=1792, T6=80, CM=96, XX=192, MN=80, T1=32)
 _sb(B, FT=1024, FU=1024, Z=1024, ET=512, RT=512)
 _sb(F, AR=32, RW=32, EC=256, EP=48, EF=256, PK=96)
-_sb(U, EP16=16, EO=32, LS=144, LL=144, R16=16, NI16=16, M16=16, J16=16, L16=16)
+_sb(U, EP16=16, EO=32, LS=144, LL=144, R16=16, NI16=16, M16=32, L16=16)
 _sb(B, RD=512, XR=512, RX=512)
 _sb(F, XE=256, ES=96, RS=256)
 _sb(F, CA=8, CJ=512, CF=16, QQ=176, W3=24)
 _sb(B, RP=256, TO=256, FB=128, EQM=256, CU=256, OV=256, Z2=256, GN=256)
-_sb(F, SC=16, GS=256, M1=256, Y0=256, NS=256, SM=160, YA=256, YB=256, YX=352, NR=256, LW=16, YO=256)
+_sb(F, SC=16, GS=256, M1=256, Y0=256, NS=256, SM=160, YA=256, YB=256, YX=352, NR=256, CL=48, YO=256)
 for _i in range(8):
     SCRATCH["P%d" % _i] = ("psum", [128, 512], F)
 PS = ["P%d" % i for i in range(8)]
@@ -182,6 +182,8 @@ def rank_program(g, core, T, topo):
     iota(["CW"], T.CW[:], [[16, 16]], 0, 0)
     iota(["CT0"], T.CT[:], [[32, 8], [0, 2]], 0, 0)
     iota(["CY"], T.CY[:], [[1, 368]], -112, 0)
+    fill(["T128"], T.TK[:, 4096:4608], 128.0)
+    fill(["T256"], T.TK[:, 4608:5120], 256.0)
     cp(["OI"], ["OU"], T.OU[:], T.OI[:])
     ts(["PC"], ["PI"], T.PI[:, 0:1], T.PC[:], 15, OP.bitwise_and)
     ts(["PC"], ["PI1"], T.PI[:, 1:2], T.PC[:], 4, OP.arith_shift_right)
@@ -191,6 +193,15 @@ def rank_program(g, core, T, topo):
     cp(["PI2"], ["m1"], T.PF[:, 2:3], T.PI[:, 2:3])
     ts(["m1"], ["m0"], T.PF[:, 3:4], T.PF[:, 2:3], -1.0, OP.mult, 1.0, OP.add)
     ts(["q"], ["qn"], T.PF[:, 4:5], T.PF[:, 0:1], -1.0, OP.mult, -0.5, OP.add)
+    ts(["BK", "g"], ["TKS"], T.TK[:, 2048:2560], T.BK[:], T.PF[:, 1:2], OP.is_equal)
+    emit("G", ["T256"], ["TKB"], lambda e: e.affine_select(
+        T.TK[:, 2560:3072], T.TK[:, 4608:5120], [[0, 128], [-1, 4]], OP.is_gt, 0.0, 2, 0))
+    for i in (2, 3):
+        emit("G", ["TKS"], ["TKT%d" % i], lambda e: e.affine_select(
+            T.TK[:, 2048 + 512 * i:2560 + 512 * i], T.TK[:, 2048:2560], [[0, 128], [1, 4]], OP.is_equal, 0.0, -i, 0))
+    for b in range(4):
+        emit("G", ["T128"], ["TK%d" % b], lambda e: e.affine_select(
+            T.TK[:, 512 * b:512 * b + 512], T.TK[:, 4096:4608], [[-1, 128], [1000, 4]], OP.is_equal, 0.0, -1000 * b, 1))
     ts(["IR", "q"], ["RQ"], T.RQ[:], T.IR[:], T.PF[:, 0:1], OP.subtract)
     ts(["RQ"], ["ME"], T.ME[:], T.RQ[:], 0.0, OP.is_equal)
     ts(["IR"], ["KP"], T.KP[:], T.IR[:], 0.5, OP.is_gt)
@@ -209,30 +220,23 @@ def rank_program(g, core, T, topo):
     ts(["RQ"], ["BS"], T.BS[:], T.RQ[:], 0.0, OP.is_ge, -2.0 ** 90, OP.mult)
     ts(["RQ"], ["BE"], T.BE[:], T.RQ[:], 0.0, OP.is_ge, 2.0 ** 90, OP.mult)
     ts(["TI"], ["TR"], T.TR[:], T.TI[:], 0.0, OP.is_le)
-    fill(["TK"], T.TK[:], 0.0)
     for a in range(4):
-        fill(["CT2"], T.CT2[:, 1024 * a:1024 * a + 4 * TILE_N[a]], 0.0)
-        act(["CT2"], ["CT3"], T.CT2[:, 4096 + 1024 * a:4096 + 1024 * a + 4 * TILE_N[a]],
-            T.CT2[:, 1024 * a:1024 * a + 4 * TILE_N[a]])
+        o, e = 1024 * a + 256 * a, 1024 * a + 4 * TILE_N[a]
+        fill(["CT2%d" % a], T.CT2[:, o:e], 0.0)
+        act(["CT2%d" % a], ["CT3%d" % a], T.CT2[:, 4096 + o:4096 + e], T.CT2[:, o:e])
     fill(["AR"], T.AR[:], 0.0)
     dma("S", "dPad", ["X0"], ["pad"], [(T.cL[:, 288:320].bitcast(dt.uint8), T.cX[:, 0:32].bitcast(dt.uint8)),
                                        (T.sL[:, 288:320], T.sX[:, 0:32])])
 
+    ZC = ["CT%d%d" % (i, a) for i in (2, 3) for a in range(4)]
+
     def late_constants():
-        for b in range(4):
-            o = 512 * b
-            ts(["TI", "TK"], ["TK%d" % b], T.TK[:, o + b:o + 512:4], T.TI[:], 0.0, OP.is_equal, 128.0, OP.mult)
         for b in range(4):
             quant(["TK%d" % b], "KR%d" % b, 0, 128, T.TK[:, 512 * b:512 * b + 512])
 
     def birth_constants():
-        ts(["BK", "g"], ["TKS"], T.TK[:, 2048:2560], T.BK[:], T.PF[:, 1:2], OP.is_equal)
-        for i in range(2):
-            ts(["TI", "TK"], ["TKB"], T.TK[:, 2560 + i:3072:4], T.TI[:], 0.0, OP.mult, 256.0, OP.add)
-            o = 3072 + 512 * i
-            ts(["BK", "g", "TK"], ["TKT"], T.TK[:, o + 2 + i:o + 512:4], T.BK[:, 2:512:4], T.PF[:, 1:2], OP.is_equal)
         for i, k in enumerate(("KS", "KB", "KT", "KU")):
-            quant(["TKS", "TKB", "TKT", "TK"], k, 0, 128, T.TK[:, 2048 + 512 * i:2560 + 512 * i])
+            quant(["TKS", "TKB", "TKT2", "TKT3"], k, 0, 128, T.TK[:, 2048 + 512 * i:2560 + 512 * i])
         ts(["CW", "xq"], ["CX"], T.CX[:], T.CW[:], T.PF[:, 5:6], OP.subtract)
         ts(["PC"], ["PI3"], T.PI[:, 3:4], T.PC[:], 31, OP.bitwise_and)
         cp(["PI3"], ["x32"], T.PF[:, 6:7], T.PI[:, 3:4])
@@ -248,12 +252,13 @@ def rank_program(g, core, T, topo):
         fill(["ZR"], T.ON[:, 32:288], 0.0)
         fill(["CM6"], T.CM[:], 0.0)
         fill(["Q4z"], T.QQ[:, 48:80], 0.0)
-        fill(["ETz"], T.ET[:], 0.0)
-        fill(["RTz"], T.RT[:], 0.0)
+        fill(["ETz"], T.ET[:, 384:512], 0.0)
+        fill(["RTz"], T.RT[:, 384:512], 0.0)
         quant(["VTL"], "V", 0, 128, T.VTL[:])
 
     ts(["CW", "q"], ["CW"], T.CW[:], T.CW[:], T.PF[:, 0:1], OP.add)
-    cp(["OL"], ["LW"], T.LW[:], T.OL[:])
+    cp(["CW"], ["CL"], T.CL[:, 0:16], T.CW[:])
+    cp(["OL"], ["LW"], T.CL[:, 16:32], T.OL[:])
     cp(["OL"], ["L16"], T.L16[:], T.OL[:])
 
     BC, BC15, BC32 = T.OU[:, 24:40], T.OU[:, 40:56], T.OU[:, 56:72]
@@ -309,14 +314,14 @@ def rank_program(g, core, T, topo):
             if m:
                 o, n = 4096 * s + 1024 * (m // 4), 64 * m
                 v = T.CT2[:, o + m % 4:o + n:4]
-                ts([bank, k, "CT2", "CT3"], ["ct%d.%d" % (s, m)], v, T[bank][:, 0:16 * m], w[:, 16 * m + 15:16 * m + 16], op)
+                ts([bank, k] + ZC, ["ct%d.%d" % (s, m)], v, T[bank][:, 0:16 * m], w[:, 16 * m + 15:16 * m + 16], op)
                 j = m % 4
                 act(["ct%d.%d" % (s, m), "AR"], ["AR%d.%d" % (s, m), "AJ%d" % j], T.AJ[:, 256 * j:256 * j + 16 * m], v,
                     AF.Copy, 0.0, 1.0, T.AR[:, 16 * s + m:16 * s + m + 1])
 
         def pair_sum(s, a):
             o, n, k, bank = 4096 * s + 1024 * a, TILE_N[a], "CD"[s] + str(a), ("P4", "P5")[s]
-            quant(["ct%d.%d" % (s, m) for m in range(4 * a, 4 * a + 4) if m] + ["CT2", "CT3"], k, 0, n, T.CT2[:, o:o + 4 * n])
+            quant(["ct%d.%d" % (s, m) for m in range(4 * a, 4 * a + 4) if m] + ZC, k, 0, n, T.CT2[:, o:o + 4 * n])
             mm([k, "KS"], bank, n, "KS", 0, k, 0, False, a == 3)
 
         def row_sum(s):
@@ -332,10 +337,6 @@ def rank_program(g, core, T, topo):
             late_constants()
         for b in range(4):
             mm(XK + ["KR%d" % b], ("P0", "P1", "P2", "P5")[b], 256, "KR%d" % b, 0, X, 0)
-        for b in range(4):
-            k = ("P0", "P1", "P2", "P5")[b]
-            act([k], ["FT%d" % b], T.FT[:, 256 * b:256 * b + 256], T[k][:, 0:256], AF.Copy, 0.0, 2.0 ** -8)
-        mm(["B", "KU"], "P5", 256, "KU", 0, "B", 0, True, False)
         pair(0, 14)
         tt(["P6", "ID"], ["V0"], T.VH[:, 1536:1792], T.P6[:, 0:256], T.ID[:], OP.add)
         pair(0, 13)
@@ -357,6 +358,11 @@ def rank_program(g, core, T, topo):
             if i == 0:
                 row_sum(0)
                 act(["RW0", "OU"], ["XR"], T.XR[:, 0:256], T.RW[:, 0:16].indirect(BC))
+        def half(b):
+            k = ("P0", "P1", "P2", "P5")[b]
+            act([k], ["FT%d" % b], T.FT[:, 256 * b:256 * b + 256], T[k][:, 0:256], AF.Copy, 0.0, 2.0 ** -8)
+        half(3)
+        mm(["B", "KU"], "P5", 256, "KU", 0, "B", 0, True, False)
         for m in range(15, 7, -1):
             pair(1, m)
         turn(["XR"], ["XS"], T.XR[:, 256:512], T.XR[:, 0:256])
@@ -368,35 +374,38 @@ def rank_program(g, core, T, topo):
                 tt(["TT", "CT"], ["T1a"], T.T1[:, 0:16], T.VT[:, 1536:1792:16], T.CT[:], OP.add)
             if m == 4:
                 tt(["T1a", "XE"], ["T1b"], T.T1[:, 16:32], T.T1[:, 0:16], T.XE[:, E15], OP.subtract)
-        for i in range(5):
-            act(["T1b"], ["T6%d" % i], T.T6[:, 16 * i:16 * i + 16], T.T1[:, 16:32], AF.Identity, 255.5 + 65536.0 * (i + 1), 256.0)
-        act(["FT0", "FT1", "FT2", "FT3"], ["FU"], T.FU[:], T.FT[:])
+                for i in range(5):
+                    act(["T1b"], ["T6%d" % i], T.T6[:, 16 * i:16 * i + 16], T.T1[:, 16:32], AF.Identity,
+                        255.5 + 65536.0 * (i + 1), 256.0)
+        for b in range(3):
+            half(b)
         for a in range(4):
             pair_sum(1, a)
-        row_sum(1)
         for i in range(6):
             turn(["VH%d" % i], ["VT%d" % i], T.VT[:, 256 * i:256 * i + 256], T.VH[:, 256 * i:256 * i + 256])
-        scan(["EX", "P5"], ["EC"], T.EC[:], T.EX[:], T.P5[:, 0:256], 0.0, OP.add, OP.max)
         VTK = ["VT%d" % i for i in range(6)]
         tt(VTK[:5] + ["T6%d" % i for i in range(5)] + ["CM6"], ["CM"], T.CM[:, 0:80], T.VT[:, 0:1280:16], T.T6[:], OP.is_gt)
-        tt(["CX", "RW1"], ["EPa"], T.EP[:, 0:16], T.CX[:], T.RW[:, 16:32], OP.subtract)
         ts(["CM", "CM6"], ["XXa"], T.XX[:, 0:96], T.CM[:], 2.0 ** 20, OP.mult)
-        tt(["EPa", "EC"], ["EP"], T.EP[:, 16:32], T.EP[:, 0:16], T.EC[:, E15], OP.add)
         tt(["XXa"] + VTK, ["XXb"], T.XX[:, 96:192], T.XX[:, 0:96], T.VT[:, 0:1536:16], OP.add)
-        cp(["EP"], ["EP16"], T.EP16[:], T.EP[:, 16:32])
         tt(["XXb"], ["MNa"], T.MN[:, 0:48], T.XX[:, 96:144], T.XX[:, 144:192], OP.min)
         tt(["MNa"], ["MNb"], T.MN[:, 48:64], T.MN[:, 0:16], T.MN[:, 16:32], OP.min)
         tt(["MNa", "MNb"], ["RI0"], T.RI[:, 0:16], T.MN[:, 48:64], T.MN[:, 32:48], OP.min)
         ts(["RI0"], ["RI1"], T.RI[:, 16:32], T.RI[:, 0:16], 255, OP.bitwise_and)
         cp(["RI1"], ["RI2"], T.EP[:, 32:48], T.RI[:, 16:32])
         act(["RI2", "OU"], ["RX"], T.RX[:, 0:256], T.EP[:, 32:48].indirect(BC))
-        cp(["ID", "EP16"], ["EF"], T.EF[:, 0:256].indirect(T.EP16[:]), T.ID[:])
+        row_sum(1)
+        cp(["FT0", "FT1", "FT2", "FT3"], ["FU"], T.FU[:], T.FT[:])
         turn(["RX"], ["RY"], T.RX[:, 256:512], T.RX[:, 0:256])
         scan(["EX", "RY"], ["RS"], T.RS[:], T.EX[:], T.RX[:, 256:512], 0.0, OP.add, OP.max)
         ts(["RS", "xq"], ["R16"], T.R16[:], T.RS[:, E15], T.PF[:, 5:6], OP.subtract)
         for z in range(8):
             act(["CB", "R16"], ["CJ%d" % (z % 2), "CA%d" % z], T.CJ[:, 256 * (z % 2):256 * (z % 2) + 256], T.CB[:, 112 - 16 * z:368 - 16 * z].indirect(T.R16[:]),
                 AF.Copy, 0.0, 1.0, T.CA[:, z:z + 1])
+        scan(["EX", "P5"], ["EC"], T.EC[:], T.EX[:], T.P5[:, 0:256], 0.0, OP.add, OP.max)
+        tt(["CX", "RW1"], ["EPa"], T.EP[:, 0:16], T.CX[:], T.RW[:, 16:32], OP.subtract)
+        tt(["EPa", "EC"], ["EP"], T.EP[:, 16:32], T.EP[:, 0:16], T.EC[:, E15], OP.add)
+        cp(["EP"], ["EP16"], T.EP16[:], T.EP[:, 16:32])
+        cp(["ID", "EP16"], ["EF"], T.EF[:, 0:256].indirect(T.EP16[:]), T.ID[:])
         for b in range(4):
             f = T.FT[:, 256 * b:256 * b + 256]
             tt(["FT%d" % b, "FU", "R16"], ["Z%d" % b], T.Z[:, b:1024:4], f.indirect(T.R16[:]),
@@ -470,7 +479,7 @@ def rank_program(g, core, T, topo):
         tt(["M1", "ID"], ["Y0"], T.Y0[:], T.M1[:], T.ID[:], OP.max)
         scan(["EX", "Y0"], ["NSx"], T.NS[:], T.EX[:], T.Y0[:], 0.0, OP.add, OP.max)
         ts(["NSx", "xq"], ["NI16"], T.NI16[:], T.NS[:, E15], T.PF[:, 5:6], OP.subtract)
-        ts(["NSx", "xq"], ["NS"], T.SM[:, 128:144], T.NS[:, E15], T.PF[:, 5:6], OP.subtract)
+        ts(["NSx", "xq"], ["NS"], T.CL[:, 32:48], T.NS[:, E15], T.PF[:, 5:6], OP.subtract)
         for b in range(4):
             k = PS[b]
             mm(["L%d" % t, "pad", "W"], k, 128, "W", 128 * b, "L", lo, True, False)
@@ -485,25 +494,21 @@ def rank_program(g, core, T, topo):
             T.cX[:, 256 * t + 256:256 * t + 512].bitcast(dt.uint32), T.cP[:, :].bitcast(dt.uint32).indirect(T.NI16[:])))
         emit("A", ["P", "Pb", "NI16"], [XN + "s"], lambda e: e.activation(
             T.sX[:, 256 * t + 256:256 * t + 512], T.sP[:, :].indirect(T.NI16[:]), AF.Copy))
-        res = T.SM[:, 128:144]
         sm = [T.SM[:, 16 * i:16 * i + 16] for i in range(8)]
-        ts(["NS"], ["GW"], sm[0], res, 256.0, OP.is_ge)
-        tt(["LW", "CW"], ["D1"], sm[1], T.LW[:], T.CW[:], OP.subtract)
-        tt(["NS", "LW"], ["E1x"], sm[2], res, T.LW[:], OP.subtract)
-        tt(["GW", "D1"], ["D2"], sm[3], sm[0], sm[1], OP.mult)
-        tt(["GW", "E1x"], ["E2x"], sm[4], sm[0], sm[2], OP.mult)
-        tt(["D2", "CW"], ["D3"], sm[5], sm[3], T.CW[:], OP.add)
-        tt(["E2x", "LW"], ["E3"], sm[6], sm[4], T.LW[:], OP.add)
-        cp(["D3"], ["M16"], T.M16[:], sm[5])
-        cp(["E3"], ["J16"], T.J16[:], sm[6])
+        ts(["NS"], ["GW"], T.SM[:, 0:16], T.CL[:, 32:48], 256.0, OP.is_ge)
+        ts(["NS"], ["GW2"], T.SM[:, 16:32], T.CL[:, 32:48], 256.0, OP.is_ge)
+        tt(["NS", "LW", "CL"], ["D1"], T.SM[:, 32:64], T.CL[:, 16:48], T.CL[:, 0:32], OP.subtract)
+        tt(["GW", "GW2", "D1"], ["D2"], T.SM[:, 64:96], T.SM[:, 0:32], T.SM[:, 32:64], OP.mult)
+        tt(["D2", "LW", "CL"], ["D3"], T.SM[:, 96:128], T.SM[:, 64:96], T.CL[:, 0:32], OP.add)
+        cp(["D3"], ["M16"], T.M16[:], T.SM[:, 96:128])
 
         def chain(t=t):
             src, k = T.Y0, "Y0"
             for i in range(5):
                 dst, kd = ((T.YA, "YA"), (T.YB, "YB"))[i % 2] if i < 4 else (T.YX, "YX")
-                act([k, "M16"], [kd], dst[:, 0:256], src[:, 0:256].indirect(T.M16[:]))
+                act([k, "M16"], [kd], dst[:, 0:256], src[:, 0:256].indirect(T.M16[:, 0:16]))
                 src, k = dst, kd
-            act(["YX", "YXe", "J16"], ["M1"], T.M1[:], T.YX[:].indirect(T.J16[:]))
+            act(["YX", "YXe", "M16"], ["M1"], T.M1[:], T.YX[:].indirect(T.M16[:, 16:32]))
 
         def unpack(t=t):
             LL = "LL%d" % t
@@ -519,8 +524,8 @@ def rank_program(g, core, T, topo):
             ts(["NR"], ["FL"], sm[0], r, 256.0, OP.is_ge)
             tt(["CW", "NR"], ["G1"], sm[1], T.CW[:], r, OP.subtract)
             tt(["FL", "G1"], ["G2"], sm[2], sm[0], sm[1], OP.mult)
-            tt(["G2", "NR"], ["LW"], T.LW[:], sm[2], r, OP.add)
-            cp(["LW"], ["L16"], T.L16[:], T.LW[:])
+            tt(["G2", "NR"], ["LW"], T.CL[:, 16:32], sm[2], r, OP.add)
+            cp(["LW"], ["L16"], T.L16[:], T.CL[:, 16:32])
         pending = [unpack, chain, relink]
 
     mm(["V", "X3", "X3s"], "P7", 256, "V", 0, "X3", 0)

@@ -40,7 +40,7 @@ _sb(B, RD=512, XR=512, RX=512)
 _sb(F, XE=256, ES=96, RS=256)
 _sb(F, CA=8, CJ=512, CF=16, QQ=176, W3=24)
 _sb(B, RP=256, TO=256, FB=128, EQM=256, CU=256, OV=256, Z2=256, GN=256)
-_sb(F, SC=16, GS=256, M1=256, Y0=256, NS=256, SM=160, YA=256, YB=256, YX=352, NR=256, CL=48, YO=256)
+_sb(F, SC=16, GS=256, M1=256, Y0=256, NS=256, SM=208, YA=256, YB=256, YX=352, NR=256, CL=48, YO=256)
 for _i in range(8):
     SCRATCH["P%d" % _i] = ("psum", [128, 512], F)
 PS = ["P%d" % i for i in range(8)]
@@ -55,6 +55,24 @@ for _i in range(3):
     PLACE["E%d" % _i] = ("E", 128 * _i)
 for _i, _k in enumerate(("KS", "KB", "KT", "KU")):
     PLACE[_k] = ("K", 512 + 128 * _i)
+WAKE, SLACK, FLIGHT = 0.2, 0.1, 4.5
+LONG = {"MS": .25, "MSE": .25, "SWS": .25, "SWE": .25, "SG": .25, "EG": .25, "V0": .25, "TT": .25, "VT": .25, "XE": .25,
+        "EC": .25, "RS": .25, "NSx": .25, "GS": .25, "NRx": .25, "BTe": .37, "BTf": .37, "Z": .37, "BTa": .13, "BTb": .13,
+        "BTc": .13, "BTd": .13, "EF": .8, "XS": .13, "RY": .13, "TO": .13, "EQM": .13, "CU": .13, "OV": .13, "GN": .13,
+        "Zx": .45, "Y0": .45, "RD": .13, "FU": .45, "X": .36, "Xs": .36, "VH": .37, "CJ": .39, "CA": .39, "FT": .23,
+        "XR": .36, "RX": .36, "ET": .2, "RP": .36, "YA": .36, "YB": .36, "YX": .36, "M": .3, "TH": .13, "AC": .25,
+        "P": .24, "Pb": .13, "B": .24, "C": .17, "D": .17, "E": .13, "RT": .1, "TKS": .45, "TKB": 1.2, "TKT": 1.2, "TK": 1.2,
+        "IR": .6, "ID": .6, "BK": 1.0, "CY": .8, "RQ": .23, "ME": .23, "KP": .23, "BS": .23, "BE": .23, "EX": .3, "CB": .3}
+
+
+def duration(q, key):
+    if q == "P":
+        return 0.2
+    if q == "G" and key[:3] == "snd":
+        return 0.7
+    if key[:2] == "ct" or key[:2] == "AR" and "." in key:
+        return 0.02 + 0.00083 * max(64, 16 * int(key.split(".")[1]))
+    return LONG.get(key.rstrip("0123456789s") or key, LONG.get(key.rstrip("0123456789"), 0.075))
 
 SEMAPHORES = ["sV", "sA", "sP", "sG", "dX", "dU", "dO", "dW", "dVV", "dPad", "dY", "dLk", "dOc", "ls",
               "aC0", "aC1", "aC2", "aL0", "aL1", "aL2"]
@@ -89,9 +107,8 @@ def rank_program(g, core, T, topo):
         for k in w:
             if k in lastw and not (q == "P" and lastw[k][0] == "sP"):
                 toks.append(lastw[k])
-            toks += [t for s, t in readers.get(k, {}).items() if s != me]
+            toks += [t for s, t in readers.get(k, {}).items()]
         sync(q, toks)
-        return toks
 
     def done(tok, r, w):
         for k in r:
@@ -100,21 +117,81 @@ def rank_program(g, core, T, topo):
             lastw[k] = tok
             readers[k] = {}
 
+    nodes = []
+
     def emit(q, r, w, fn):
-        deps(q, r, w)
-        s = own[q]
-        fn(eng[q]).then_inc(T.sem[s], 1)
-        cnt[s] = cnt.get(s, 0) + 1
-        clk = dict(known[q])
-        clk[s] = cnt[s]
-        done((s, cnt[s], clk), r, w)
+        def issue():
+            deps(q, r, w)
+            s = own[q]
+            fn(eng[q]).then_inc(T.sem[s], 1)
+            cnt[s] = cnt.get(s, 0) + 1
+            clk = dict(known[q])
+            clk[s] = cnt[s]
+            done((s, cnt[s], clk), r, w)
+        nodes.append((q, r, w, issue, duration(q, w[0]), 0.0))
 
     def dma(q, s, r, w, pairs):
-        deps(q, r, w)
-        for o, i in pairs:
-            eng[q].dma_start(o, i).then_inc(T.sem[s], 16)
-            cnt[s] = cnt.get(s, 0) + 16
-        done((s, cnt[s], dict(known[q])), r, w)
+        def issue():
+            deps(q, r, w)
+            for o, i in pairs:
+                eng[q].dma_start(o, i).then_inc(T.sem[s], 16)
+                cnt[s] = cnt.get(s, 0) + 16
+            done((s, cnt[s], dict(known[q])), r, w)
+        nodes.append((q, r, w, issue, 0.1, 2.0))
+
+    def arrival(key, r, tok):
+        nodes.append(("R", r, [key], lambda: done(tok, [], [key]), 0.0, FLIGHT))
+
+    def schedule():
+        n = len(nodes)
+        succ, left = [[] for _ in range(n)], [0] * n
+        wr, rd = {}, {}
+
+        def edge(a, b, lag):
+            if a != b:
+                succ[a].append((b, lag))
+                left[b] += 1
+        for i, (q, r, w, fn, c, late) in enumerate(nodes):
+            for k in r:
+                if k in wr:
+                    edge(wr[k], i, 0.0 if q == "P" and nodes[wr[k]][0] == "P" else WAKE)
+                if k in PS:
+                    for j in rd.get(k, []):
+                        if nodes[j][0] != q:
+                            edge(j, i, WAKE)
+            for k in w:
+                if k in wr:
+                    edge(wr[k], i, 0.0 if q == "P" and nodes[wr[k]][0] == "P" else WAKE)
+                for j in rd.get(k, []):
+                    edge(j, i, WAKE)
+            for k in r:
+                rd.setdefault(k, []).append(i)
+            for k in w:
+                wr[k], rd[k] = i, []
+        rest = [0.0] * n
+        for i in range(n - 1, -1, -1):
+            rest[i] = nodes[i][4] + nodes[i][5] + max([lag + rest[j] for j, lag in succ[i]] + [0.0])
+        ready, free, todo = [0.0] * n, {}, [i for i in range(n) if not left[i]]
+        while todo:
+            best = None
+            for i in todo:
+                at = max(ready[i], free.get(nodes[i][0], 0.0))
+                if best is None or (at, -rest[i]) < best[:2]:
+                    best = (at, -rest[i], i)
+            at, i = best[0], best[2]
+            for j in todo:
+                if nodes[j][0] == nodes[i][0] and max(ready[j], free.get(nodes[j][0], 0.0)) <= at + SLACK and rest[j] > rest[i]:
+                    i = j
+            at = max(ready[i], free.get(nodes[i][0], 0.0))
+            todo.remove(i)
+            nodes[i][3]()
+            end = at + nodes[i][4]
+            free[nodes[i][0]] = end
+            for j, lag in succ[i]:
+                ready[j] = max(ready[j], (at if lag == 0.0 and nodes[j][0] == nodes[i][0] else end + nodes[i][5]) + lag)
+                left[j] -= 1
+                if not left[j]:
+                    todo.append(j)
 
     def tt(r, w, out, a, b, op):
         emit("V", r, w, lambda e: e.tensor_tensor(out, a, b, op))
@@ -197,18 +274,27 @@ def rank_program(g, core, T, topo):
     emit("G", ["T256"], ["TKB"], lambda e: e.affine_select(
         T.TK[:, 2560:3072], T.TK[:, 4608:5120], [[0, 128], [-1, 4]], OP.is_gt, 0.0, 2, 0))
     for i in (2, 3):
-        emit("G", ["TKS"], ["TKT%d" % i], lambda e: e.affine_select(
+        emit("G", ["TKS"], ["TKT%d" % i], lambda e, i=i: e.affine_select(
             T.TK[:, 2048 + 512 * i:2560 + 512 * i], T.TK[:, 2048:2560], [[0, 128], [1, 4]], OP.is_equal, 0.0, -i, 0))
     for b in range(4):
-        emit("G", ["T128"], ["TK%d" % b], lambda e: e.affine_select(
+        emit("G", ["T128"], ["TK%d" % b], lambda e, b=b: e.affine_select(
             T.TK[:, 512 * b:512 * b + 512], T.TK[:, 4096:4608], [[-1, 128], [1000, 4]], OP.is_equal, 0.0, -1000 * b, 1))
-    ts(["IR", "q"], ["RQ"], T.RQ[:], T.IR[:], T.PF[:, 0:1], OP.subtract)
-    ts(["RQ"], ["ME"], T.ME[:], T.RQ[:], 0.0, OP.is_equal)
-    ts(["IR"], ["KP"], T.KP[:], T.IR[:], 0.5, OP.is_gt)
-    ts(["RQ"], ["BE"], T.BE[:], T.RQ[:], 0.0, OP.is_gt, 512.0, OP.mult)
-    ts(["ME"], ["EX"], T.EX[:], T.ME[:], -2.0 ** 20, OP.mult)
-    tt(["BE", "EX"], ["EX"], T.EX[:], T.BE[:], T.EX[:], OP.add)
+    ts(["q"], ["nq"], T.PF[:, 12:13], T.PF[:, 0:1], -1.0, OP.mult)
+    act(["IR", "nq"], ["RQ"], T.RQ[:], T.IR[:], AF.Identity, T.PF[:, 12:13])
+    act(["RQ"], ["BS"], T.BS[:], T.RQ[:], AF.Abs)
+    act(["BS"], ["ME"], T.ME[:], T.BS[:], AF.Relu, 1.0, -1.0)
+    act(["IR"], ["KP"], T.KP[:], T.IR[:], AF.Sign)
+    act(["RQ"], ["BE"], T.BE[:], T.RQ[:], AF.Sign, 0.5)
+    act(["BE"], ["BE"], T.BE[:], T.BE[:], AF.Relu)
+    act(["BE"], ["BS"], T.BS[:], T.BE[:], AF.Copy, 0.0, -2.0 ** 90)
+    act(["BE"], ["RQ"], T.RQ[:], T.BE[:], AF.Copy, 0.0, 512.0)
+    act(["ME"], ["EX"], T.EX[:], T.ME[:], AF.Copy, 0.0, -2.0 ** 20)
+    tt(["RQ", "EX"], ["EX"], T.EX[:], T.RQ[:], T.EX[:], OP.add)
+    act(["BE"], ["BE"], T.BE[:], T.BE[:], AF.Copy, 0.0, 2.0 ** 90)
+    act(["TI"], ["TR"], T.TR[:], T.TI[:], AF.Sign, 0.5, -1.0)
+    act(["TR"], ["TR"], T.TR[:], T.TR[:], AF.Relu)
     ts(["q"], ["xq"], T.PF[:, 5:6], T.PF[:, 0:1], -512.0, OP.mult, 7680.0, OP.add)
+    ts(["xq"], ["nxq"], T.PF[:, 14:15], T.PF[:, 5:6], -1.0, OP.mult)
     for i in range(4):
         ts(["xq"], ["xq4"], T.PF[:, 8 + i:9 + i], T.PF[:, 5:6], -4.0, OP.mult, float(i), OP.add)
     quant(["UT"], "U", 0, 128, T.UT[:, 0:512])
@@ -217,9 +303,6 @@ def rank_program(g, core, T, topo):
     emit("V", ["U", "OU"], ["UPs"], lambda e: e.tensor_copy(T.sUP[:, 0:384], T.sU[:, 0:128].indirect(T.OU[:, 0:24])))
     UPK = ["UPc", "UPs"]
     quant(["XT"], "X0", 0, 256, T.XT[:])
-    ts(["RQ"], ["BS"], T.BS[:], T.RQ[:], 0.0, OP.is_ge, -2.0 ** 90, OP.mult)
-    ts(["RQ"], ["BE"], T.BE[:], T.RQ[:], 0.0, OP.is_ge, 2.0 ** 90, OP.mult)
-    ts(["TI"], ["TR"], T.TR[:], T.TI[:], 0.0, OP.is_le)
     for a in range(4):
         o, e = 1024 * a + 256 * a, 1024 * a + 4 * TILE_N[a]
         fill(["CT2%d" % a], T.CT2[:, o:e], 0.0)
@@ -244,9 +327,11 @@ def rank_program(g, core, T, topo):
         ts(["CT0", "x32q"], ["CT"], T.CT[:], T.CT[:], T.PF[:, 7:8], OP.add)
 
     def count_constants():
-        ts(["CY", "q"], ["CY"], T.CY[:], T.CY[:], T.PF[:, 0:1], OP.subtract)
-        ts(["CY"], ["CB"], T.CB[:], T.CY[:], 128.0, OP.is_equal, 512.0, OP.mult)
-        ts(["CY"], ["CY"], T.CY[:], T.CY[:], 0.0, OP.is_equal)
+        ts(["nq"], ["nq128"], T.PF[:, 13:14], T.PF[:, 12:13], -128.0, OP.add)
+        act(["CY", "nq128"], ["CB"], T.CB[:], T.CY[:], AF.Abs, T.PF[:, 13:14])
+        act(["CB"], ["CB"], T.CB[:], T.CB[:], AF.Relu, 512.0, -512.0)
+        act(["CY", "nq"], ["CY"], T.CY[:], T.CY[:], AF.Abs, T.PF[:, 12:13])
+        act(["CY"], ["CY"], T.CY[:], T.CY[:], AF.Relu, 1.0, -1.0)
         tt(["CY", "CB"], ["CB"], T.CB[:], T.CB[:], T.CY[:], OP.add)
         fill(["ON"], T.ON[:, 0:32], 1.0)
         fill(["ZR"], T.ON[:, 32:288], 0.0)
@@ -270,9 +355,11 @@ def rank_program(g, core, T, topo):
     sent = [0]
 
     def send(r, out, src, rsem):
-        deps("G", r, [])
-        g.remote_dma(out, src, T.sem[rsem], T.sem.ls, pid, rid, mask)
-        sent[0] += n_eng
+        def issue():
+            deps("G", r, [])
+            g.remote_dma(out, src, T.sem[rsem], T.sem.ls, pid, rid, mask)
+            sent[0] += n_eng
+        nodes.append(("G", r, ["snd" + rsem], issue, 0.7, 0.0))
 
     pending = []
 
@@ -290,7 +377,7 @@ def rank_program(g, core, T, topo):
         tt(["P7", "ME"], ["MS"], T.MS[:, 0:256], T.P7[:, 0:256], T.ME[:], OP.mult)
         if t == 0:
             birth_constants()
-        ts(["DL"], ["DL2"], T.DL[:, 2:4], T.DL[:, 0:2], 2.0 ** -120, OP.add)
+        act(["DL"], ["DL2"], T.DL[:, 2:4], T.DL[:, 0:2], AF.Identity, 2.0 ** -120)
         for h in range(2):
             act(["TR", "DL2", "SB0", "SB1"], ["TH%d" % h], T["TH%d" % h][:], T.TR[:], AF.Identity,
                 T.SB2[:, h:h + 1], T.DL[:, 2 + h:3 + h])
@@ -385,7 +472,7 @@ def rank_program(g, core, T, topo):
             turn(["VH%d" % i], ["VT%d" % i], T.VT[:, 256 * i:256 * i + 256], T.VH[:, 256 * i:256 * i + 256])
         VTK = ["VT%d" % i for i in range(6)]
         tt(VTK[:5] + ["T6%d" % i for i in range(5)] + ["CM6"], ["CM"], T.CM[:, 0:80], T.VT[:, 0:1280:16], T.T6[:], OP.is_gt)
-        ts(["CM", "CM6"], ["XXa"], T.XX[:, 0:96], T.CM[:], 2.0 ** 20, OP.mult)
+        act(["CM", "CM6"], ["XXa"], T.XX[:, 0:96], T.CM[:], AF.Copy, 0.0, 2.0 ** 20)
         tt(["XXa"] + VTK, ["XXb"], T.XX[:, 96:192], T.XX[:, 0:96], T.VT[:, 0:1536:16], OP.add)
         tt(["XXb"], ["MNa"], T.MN[:, 0:48], T.XX[:, 96:144], T.XX[:, 144:192], OP.min)
         tt(["MNa"], ["MNb"], T.MN[:, 48:64], T.MN[:, 0:16], T.MN[:, 16:32], OP.min)
@@ -428,31 +515,30 @@ def rank_program(g, core, T, topo):
                  T.cE[:, 128 * t:128 * t + KEEP].bitcast(dt.uint8), "aC%d" % t)
             send(["E%d" % t], T.sL[:, lo:lo + KEEP], T.sE[:, 128 * t:128 * t + KEEP], "aC%d" % t)
             send(["LS%d" % t], T.LL[:, 48 * t:48 * t + 48], T.LS[:, 48 * t:48 * t + 48], "aL%d" % t)
-            lastw["L%d" % t] = ("aC%d" % t, 2 * n_arr, {})
-            lastw["LL%d" % t] = ("aL%d" % t, n_arr, {})
+            arrival("L%d" % t, ["sndaC%d" % t], ("aC%d" % t, 2 * n_arr, {}))
+            arrival("LL%d" % t, ["sndaL%d" % t], ("aL%d" % t, n_arr, {}))
         tt(["PKa", "EF"], ["PKb"], T.PK[:, 48:96], T.PK[:, 0:48], T.EF[:, 0:48], OP.add)
         quant(ZK, "P", 0, 256, T.Z[:])
         cp(["PKb"], ["LS%d" % t], T.LS[:, 48 * t:48 * t + 48], T.PK[:, 48:96])
         cp(["CA%d" % z for z in range(8)], ["CI0"], T.CI[:, 0:8], T.CA[:])
         ts(["CI0"], ["CI1"], T.CI[:, 8:16], T.CI[:, 0:8], 511, OP.bitwise_and)
         ts(["CI0"], ["CI2"], T.CI[:, 16:24], T.CI[:, 0:8], 9, OP.arith_shift_right)
-        ts(["CI1", "CI2"], ["CF"], T.CF[:], T.CI[:, 8:24], 16.0, OP.min)
         Q1, Q2, Q3, Q4, Q5, Q6, Q7 = [(a, a + 32) for a in (0, 16, 32, 48, 80, 112, 144)]
 
         def qq(q, a=0, b=32, step=1, p=0, np_=128):
             return T.QQ[p:p + np_, q[0] + a:q[0] + b:step]
-        cp(["CF"], ["Q1"], qq(Q1, 0, 16, 1, 0, 64), T.CF[64:128, :])
-        cp(["CF"], ["Q1b"], qq(Q1, 0, 16, 1, 64, 64), T.CF[0:64, :])
-        tt(["CF", "Q1", "Q1b"], ["Q2"], qq(Q2, 0, 16), T.CF[:], qq(Q1, 0, 16), OP.add)
+        cp(["CI1", "CI2"], ["Q1"], qq(Q1, 0, 16, 1, 0, 64), T.CI[64:128, 8:24])
+        cp(["CI1", "CI2"], ["Q1b"], qq(Q1, 0, 16, 1, 64, 64), T.CI[0:64, 8:24])
+        tt(["CI1", "CI2", "Q1", "Q1b"], ["Q2"], qq(Q2, 0, 16), T.CI[:, 8:24], qq(Q1, 0, 16), OP.add)
         for a in range(4):
             b = a ^ 1
-            cp(["Q2"], ["Q3%d" % a], qq(Q3, 0, 16, 1, 32 * a, 32), qq(Q2, 0, 16, 1, 32 * b, 32))
+            (cp, cp, act, act)[a](["Q2"], ["Q3%d" % a], qq(Q3, 0, 16, 1, 32 * a, 32), qq(Q2, 0, 16, 1, 32 * b, 32))
         tt(["Q2", "Q30", "Q31", "Q32", "Q33", "Q4z"], ["Q4"], qq(Q4, 0, 16), qq(Q2, 0, 16), qq(Q3, 0, 16), OP.add)
         turn(["Q4", "Q4z"], ["Q5"], qq(Q5), qq(Q4))
         tt(["Q5"], ["Q6"], qq(Q6, 0, 16), qq(Q5, 0, 16), qq(Q5, 16, 32), OP.add)
         tt(["Q5"], ["Q6b"], qq(Q6, 16, 32), qq(Q5, 0, 16), qq(Q5, 16, 32), OP.add)
         turn(["Q6", "Q6b"], ["Q7"], qq(Q7), qq(Q6))
-        ts(["Q7", "m0"], ["W3a"], T.W3[:, 0:8], qq(Q7, 0, 16, 2), T.PF[:, 3:4], OP.mult)
+        act(["Q7", "m0"], ["W3a"], T.W3[:, 0:8], qq(Q7, 0, 16, 2), AF.Copy, 0.0, T.PF[:, 3:4])
         act(["Q7", "m1"], ["W3b"], T.W3[:, 8:16], qq(Q7, 1, 16, 2), AF.Copy, 0.0, T.PF[:, 2:3])
         send_columns()
         tt(["W3a", "W3b"], ["W3"], T.W3[:, 16:24], T.W3[:, 0:8], T.W3[:, 8:16], OP.add)
@@ -463,23 +549,21 @@ def rank_program(g, core, T, topo):
         ts(["AC"], ["N1"], T.SC[:, 1:2], T.SC[:, 0:1], -0.5, OP.mult, 128.0, OP.add)
         ts(["ON", "F1"], ["FB"], T.FB[:, 0:32], T.ON[:, 0:32], T.SC[:, 2:3], OP.mult)
         ts(["AC", "N1"], ["NF"], T.SC[:, 3:4], T.SC[:, 0:1], 64.0, OP.is_gt, T.SC[:, 1:2], OP.mult)
-        ts(["ON", "NF"], ["FBb"], T.FB[:, 32:64], T.ON[:, 0:32], T.SC[:, 3:4], OP.mult)
+        act(["ON", "NF"], ["FBb"], T.FB[:, 32:64], T.ON[:, 0:32], AF.Copy, 0.0, T.SC[:, 3:4])
         turn(["FB", "FBb"], ["FX"], T.FB[:, 64:128], T.FB[:, 0:64])
         emit("V", ["FX"], ["SF"], lambda e: e.tensor_reduce(T.SC[:, 4:5], T.FB[:, 64:80], AxisListType.X, OP.add))
         emit("V", ["FX"], ["NP"], lambda e: e.tensor_reduce(T.SC[:, 5:6], T.FB[:, 96:112], AxisListType.X, OP.max))
-        ts(["SF"], ["TS"], T.SC[:, 6:7], T.SC[:, 4:5], -1.0, OP.mult, 16.0, OP.add)
-        ts(["NP"], ["ND"], T.SC[:, 7:8], T.SC[:, 5:6], -1.0, OP.mult, float(KEEP), OP.add)
-        ts(["TO", "TS"], ["EQM"], T.EQM[:], T.TO[:], T.SC[:, 6:7], OP.is_equal)
+        ts(["TO", "SF"], ["EQM"], T.EQM[:], T.TO[:], T.SC[:, 4:5], OP.add, 16.0, OP.is_equal)
         scan(["EQM", "ZR"], ["CU"], T.CU[:], T.EQM[:], T.ON[:, 32:288], 0.0, OP.add, OP.max)
-        ts(["CU", "ND"], ["OV"], T.OV[:], T.CU[:], T.SC[:, 7:8], OP.is_gt)
-        tt(["TO", "OV"], ["Z2x"], T.Z2[:], T.TO[:], T.OV[:], OP.add)
-        ts(["Z2x", "TS"], ["GN"], T.GN[:], T.Z2[:], T.SC[:, 6:7], OP.is_le)
+        ts(["CU", "NP"], ["OV"], T.OV[:], T.CU[:], T.SC[:, 5:6], OP.add, float(KEEP), OP.is_gt)
+        tt(["TO", "OV"], ["Zx"], T.Z2[:], T.TO[:], T.OV[:], OP.add)
+        ts(["Zx", "SF"], ["GN"], T.GN[:], T.Z2[:], T.SC[:, 4:5], OP.add, 16.0, OP.is_le)
         scan(["GN", "ZR"], ["GS"], T.GS[:], T.GN[:], T.ON[:, 32:288], 255.0, OP.add, OP.max)
-        tt(["GS", "GN"], ["M1"], T.M1[:], T.GS[:], T.GN[:], OP.mult)
+        scan(["GS", "GN"], ["M1"], T.M1[:], T.GS[:], T.GN[:], 0.0, OP.max, OP.mult)
         tt(["M1", "ID"], ["Y0"], T.Y0[:], T.M1[:], T.ID[:], OP.max)
         scan(["EX", "Y0"], ["NSx"], T.NS[:], T.EX[:], T.Y0[:], 0.0, OP.add, OP.max)
         ts(["NSx", "xq"], ["NI16"], T.NI16[:], T.NS[:, E15], T.PF[:, 5:6], OP.subtract)
-        ts(["NSx", "xq"], ["NS"], T.CL[:, 32:48], T.NS[:, E15], T.PF[:, 5:6], OP.subtract)
+        act(["NSx", "nxq"], ["NS"], T.CL[:, 32:48], T.NS[:, E15], AF.Identity, T.PF[:, 14:15])
         for b in range(4):
             k = PS[b]
             mm(["L%d" % t, "pad", "W"], k, 128, "W", 128 * b, "L", lo, True, False)
@@ -490,11 +574,10 @@ def rank_program(g, core, T, topo):
             ts([PS[b], "RTz"], ["RT%d" % b], T.RT[:, b:384:4], T[PS[b]][:, 0:96], 2.0 ** -7, OP.mult)
         quant(["RT0", "RT1", "RT2", "RT3", "RTz"], "P", 256, 384, T.RT[:])
         XN = "X%d" % (t + 1)
-        emit("V", ["P", "Pb", "NI16"], [XN], lambda e: e.tensor_copy(
+        emit("V", ["P", "Pb", "NI16"], [XN], lambda e, t=t: e.tensor_copy(
             T.cX[:, 256 * t + 256:256 * t + 512].bitcast(dt.uint32), T.cP[:, :].bitcast(dt.uint32).indirect(T.NI16[:])))
-        emit("A", ["P", "Pb", "NI16"], [XN + "s"], lambda e: e.activation(
+        emit("A", ["P", "Pb", "NI16"], [XN + "s"], lambda e, t=t: e.activation(
             T.sX[:, 256 * t + 256:256 * t + 512], T.sP[:, :].indirect(T.NI16[:]), AF.Copy))
-        sm = [T.SM[:, 16 * i:16 * i + 16] for i in range(8)]
         ts(["NS"], ["GW"], T.SM[:, 0:16], T.CL[:, 32:48], 256.0, OP.is_ge)
         ts(["NS"], ["GW2"], T.SM[:, 16:32], T.CL[:, 32:48], 256.0, OP.is_ge)
         tt(["NS", "LW", "CL"], ["D1"], T.SM[:, 32:64], T.CL[:, 16:48], T.CL[:, 0:32], OP.subtract)
@@ -520,7 +603,8 @@ def rank_program(g, core, T, topo):
         def relink():
             scan(["EX", "M1"], ["NRx"], T.NR[:], T.EX[:], T.M1[:], 0.0, OP.add, OP.max)
             r = T.SM[:, 144:160]
-            ts(["NRx", "xq"], ["NR"], r, T.NR[:, E15], T.PF[:, 5:6], OP.subtract)
+            sm = [T.SM[:, 160 + 16 * i:176 + 16 * i] for i in range(3)]
+            act(["NRx", "nxq"], ["NR"], r, T.NR[:, E15], AF.Identity, T.PF[:, 14:15])
             ts(["NR"], ["FL"], sm[0], r, 256.0, OP.is_ge)
             tt(["CW", "NR"], ["G1"], sm[1], T.CW[:], r, OP.subtract)
             tt(["FL", "G1"], ["G2"], sm[2], sm[0], sm[1], OP.mult)
@@ -540,6 +624,7 @@ def rank_program(g, core, T, topo):
     tt(["GS", "NRx"], ["Y0"], T.Y0[:], T.GS[:], T.NR[:], OP.mult)
     tt(["Y0", "M1"], ["NSx", "NS"], T.NS[:], T.Y0[:], T.M1[:], OP.add)
     dma("S", "dLk", ["NS"], ["lk"], [(T.lk[:, :], T.NS[0:128:16, :])])
+    schedule()
     for s in cnt:
         if known["S"].get(s, 0) < cnt[s]:
             g.sync.wait_ge(T.sem[s], cnt[s])

@@ -38,9 +38,9 @@ _sb(F, AR=32, RW=32, EC=256, EP=48, EF=256, PK=96)
 _sb(U, EP16=16, EO=32, LS=144, LL=144, R16=16, NI16=16, M16=32, L16=16)
 _sb(B, RD=512, XR=512, RX=512)
 _sb(F, XE=256, ES=96, RS=256)
-_sb(F, CA=8, CJ=512, CF=16, QQ=176, W3=24)
+_sb(F, CA=8, CJ=512, CF=16, QQ=176, W3=32)
 _sb(B, RP=256, TO=256, FB=128, EQM=256, CU=256, OV=256, Z2=256, GN=256)
-_sb(F, SC=16, GS=256, M1=256, Y0=256, NS=256, SM=208, YA=256, YB=256, YX=352, NR=256, CL=48, YO=256)
+_sb(F, SC=16, GS=256, M1=256, Y0=256, NS=256, SM=208, YA=256, YB=256, YX=352, NR=256, CL=64, YO=256)
 for _i in range(8):
     SCRATCH["P%d" % _i] = ("psum", [128, 512], F)
 PS = ["P%d" % i for i in range(8)]
@@ -55,7 +55,7 @@ for _i in range(3):
     PLACE["E%d" % _i] = ("E", 128 * _i)
 for _i, _k in enumerate(("KS", "KB", "KT", "KU")):
     PLACE[_k] = ("K", 512 + 128 * _i)
-WAKE, SLACK, FLIGHT = 0.2, 0.1, 4.5
+WAKE, SLACK, FLIGHT = 0.3, 0.25, 4.5
 LONG = {"MS": .25, "MSE": .25, "SWS": .25, "SWE": .25, "SG": .25, "EG": .25, "V0": .25, "TT": .25, "VT": .25, "XE": .25,
         "EC": .25, "RS": .25, "NSx": .25, "GS": .25, "NRx": .25, "BTe": .37, "BTf": .37, "Z": .37, "BTa": .13, "BTb": .13,
         "BTc": .13, "BTd": .13, "EF": .8, "XS": .13, "RY": .13, "TO": .13, "EQM": .13, "CU": .13, "OV": .13, "GN": .13,
@@ -251,7 +251,7 @@ def rank_program(g, core, T, topo):
     iotai(["OI"], T.OI[:, 16:24], [[0, 8]], 8, 0)
     iotai(["OI"], T.OI[:, 24:40], [[1, 16]], 0, 0)
     iotai(["OI"], T.OI[:, 40:56], [[16, 16]], 15, 0)
-    iotai(["OI"], T.OI[:, 56:72], [[1, 8], [0, 2]], 0, 0)
+    iotai(["OI2"], T.OI[:, 56:72], [[2, 8], [0, 2]], 0, 0)
     iota(["IR"], T.IR[:], [[0, 16], [1, 16]], 0, 0)
     iota(["TI"], T.TI[:], [[1, 128]], 0, -1)
     iota(["ID"], T.ID[:], [[1, 256]], 0, 0)
@@ -259,16 +259,16 @@ def rank_program(g, core, T, topo):
     iota(["CW"], T.CW[:], [[16, 16]], 0, 0)
     iota(["CT0"], T.CT[:], [[32, 8], [0, 2]], 0, 0)
     iota(["CY"], T.CY[:], [[1, 368]], -112, 0)
-    fill(["T128"], T.TK[:, 4096:4608], 128.0)
+    iota(["T128"], T.TK[:, 4096:4608], [[0, 512]], 128, 0)
     fill(["T256"], T.TK[:, 4608:5120], 256.0)
-    cp(["OI"], ["OU"], T.OU[:], T.OI[:])
+    cp(["OI"], ["OU"], T.OU[:, 0:56], T.OI[:, 0:56])
     ts(["PC"], ["PI"], T.PI[:, 0:1], T.PC[:], 15, OP.bitwise_and)
     ts(["PC"], ["PI1"], T.PI[:, 1:2], T.PC[:], 4, OP.arith_shift_right)
     ts(["PI1"], ["PI2"], T.PI[:, 2:3], T.PI[:, 1:2], 1, OP.bitwise_and)
     cp(["PI"], ["q"], T.PF[:, 0:1], T.PI[:, 0:1])
     cp(["PI1"], ["g"], T.PF[:, 1:2], T.PI[:, 1:2])
     cp(["PI2"], ["m1"], T.PF[:, 2:3], T.PI[:, 2:3])
-    ts(["m1"], ["m0"], T.PF[:, 3:4], T.PF[:, 2:3], -1.0, OP.mult, 1.0, OP.add)
+    ts(["OI2", "m1"], ["OU2"], T.OU[:, 56:72], T.OI[:, 56:72], T.PF[:, 2:3], OP.add)
     ts(["q"], ["qn"], T.PF[:, 4:5], T.PF[:, 0:1], -1.0, OP.mult, -0.5, OP.add)
     ts(["BK", "g"], ["TKS"], T.TK[:, 2048:2560], T.BK[:], T.PF[:, 1:2], OP.is_equal)
     emit("G", ["T256"], ["TKB"], lambda e: e.affine_select(
@@ -300,7 +300,8 @@ def rank_program(g, core, T, topo):
     quant(["UT"], "U", 0, 128, T.UT[:, 0:512])
     emit("V", ["U", "OU"], ["UPc"], lambda e: e.tensor_copy(
         T.cUP[:, 0:384].bitcast(dt.uint32), T.cU[:, 0:128].bitcast(dt.uint32).indirect(T.OU[:, 0:24])))
-    emit("V", ["U", "OU"], ["UPs"], lambda e: e.tensor_copy(T.sUP[:, 0:384], T.sU[:, 0:128].indirect(T.OU[:, 0:24])))
+    emit("A", ["U", "OU"], ["UPs"], lambda e: e.activation(
+        T.sUP[:, 0:384], T.sU[:, 0:128].indirect(T.OU[:, 0:24]), AF.Copy))
     UPK = ["UPc", "UPs"]
     quant(["XT"], "X0", 0, 256, T.XT[:])
     for a in range(4):
@@ -321,6 +322,7 @@ def rank_program(g, core, T, topo):
         for i, k in enumerate(("KS", "KB", "KT", "KU")):
             quant(["TKS", "TKB", "TKT2", "TKT3"], k, 0, 128, T.TK[:, 2048 + 512 * i:2560 + 512 * i])
         ts(["CW", "xq"], ["CX"], T.CX[:], T.CW[:], T.PF[:, 5:6], OP.subtract)
+        ts(["CW", "xq"], ["CP"], T.W3[:, 16:32], T.CW[:], T.PF[:, 5:6], OP.add)
         ts(["PC"], ["PI3"], T.PI[:, 3:4], T.PC[:], 31, OP.bitwise_and)
         cp(["PI3"], ["x32"], T.PF[:, 6:7], T.PI[:, 3:4])
         ts(["x32", "xq"], ["x32q"], T.PF[:, 7:8], T.PF[:, 6:7], T.PF[:, 5:6], OP.add)
@@ -448,6 +450,7 @@ def rank_program(g, core, T, topo):
         def half(b):
             k = ("P0", "P1", "P2", "P5")[b]
             act([k], ["FT%d" % b], T.FT[:, 256 * b:256 * b + 256], T[k][:, 0:256], AF.Copy, 0.0, 2.0 ** -8)
+            act([k], ["FU%d" % b], T.FU[:, 256 * b:256 * b + 256], T[k][:, 0:256], AF.Copy, 0.0, 2.0 ** -8)
         half(3)
         mm(["B", "KU"], "P5", 256, "KU", 0, "B", 0, True, False)
         for m in range(15, 7, -1):
@@ -481,7 +484,6 @@ def rank_program(g, core, T, topo):
         cp(["RI1"], ["RI2"], T.EP[:, 32:48], T.RI[:, 16:32])
         act(["RI2", "OU"], ["RX"], T.RX[:, 0:256], T.EP[:, 32:48].indirect(BC))
         row_sum(1)
-        cp(["FT0", "FT1", "FT2", "FT3"], ["FU"], T.FU[:], T.FT[:])
         turn(["RX"], ["RY"], T.RX[:, 256:512], T.RX[:, 0:256])
         scan(["EX", "RY"], ["RS"], T.RS[:], T.EX[:], T.RX[:, 256:512], 0.0, OP.add, OP.max)
         ts(["RS", "xq"], ["R16"], T.R16[:], T.RS[:, E15], T.PF[:, 5:6], OP.subtract)
@@ -495,7 +497,7 @@ def rank_program(g, core, T, topo):
         cp(["ID", "EP16"], ["EF"], T.EF[:, 0:256].indirect(T.EP16[:]), T.ID[:])
         for b in range(4):
             f = T.FT[:, 256 * b:256 * b + 256]
-            tt(["FT%d" % b, "FU", "R16"], ["Z%d" % b], T.Z[:, b:1024:4], f.indirect(T.R16[:]),
+            tt(["FT%d" % b, "FU%d" % b, "R16"], ["Z%d" % b], T.Z[:, b:1024:4], f.indirect(T.R16[:]),
                T.FU[:, 256 * b:256 * b + 256], OP.add)
             if b == 1:
                 scan(["EX", "EF"], ["ES"], T.ES[:], T.EX[:, 0:96], T.EF[:, 0:96], 0.0, OP.add, OP.max)
@@ -505,7 +507,7 @@ def rank_program(g, core, T, topo):
                        T.PF[:, 8 + i:9 + i], OP.add)
         ZK = ["Z0", "Z1", "Z2", "Z3"]
         for b in range(4):
-            act(ZK + ["EO%d" % b], ["ET%d" % b], T.ET[:, b:384:4], T.Z[:].indirect(T.EO[:, 8 * b:8 * b + 6]))
+            (cp, cp, act, act)[b](ZK + ["EO%d" % b], ["ET%d" % b], T.ET[:, b:384:4], T.Z[:].indirect(T.EO[:, 8 * b:8 * b + 6]))
         act(["EF"], ["PKa"], T.PK[:, 0:48], T.EF[:, 48:96], AF.Copy, 0.0, 256.0)
         lo = KEEP * (ROUNDS - 1 - t)
 
@@ -538,32 +540,27 @@ def rank_program(g, core, T, topo):
         tt(["Q5"], ["Q6"], qq(Q6, 0, 16), qq(Q5, 0, 16), qq(Q5, 16, 32), OP.add)
         tt(["Q5"], ["Q6b"], qq(Q6, 16, 32), qq(Q5, 0, 16), qq(Q5, 16, 32), OP.add)
         turn(["Q6", "Q6b"], ["Q7"], qq(Q7), qq(Q6))
-        act(["Q7", "m0"], ["W3a"], T.W3[:, 0:8], qq(Q7, 0, 16, 2), AF.Copy, 0.0, T.PF[:, 3:4])
-        act(["Q7", "m1"], ["W3b"], T.W3[:, 8:16], qq(Q7, 1, 16, 2), AF.Copy, 0.0, T.PF[:, 2:3])
         send_columns()
-        tt(["W3a", "W3b"], ["W3"], T.W3[:, 16:24], T.W3[:, 0:8], T.W3[:, 8:16], OP.add)
-        act(["W3", "OU"], ["RP"], T.RP[:], T.W3[:, 16:24].indirect(BC32))
+        act(["Q7", "OU2"], ["RP"], T.RP[:], qq(Q7).indirect(BC32))
         turn(["RP"], ["TO"], T.TO[:], T.RP[:])
         act(["TO", "qn"], ["AJ0", "AC"], T.AJ[:, 0:256], T.TO[:], AF.Sign, T.PF[:, 4:5], 1.0, T.SC[:, 0:1])
         ts(["AC"], ["F1"], T.SC[:, 2:3], T.SC[:, 0:1], 64.0, OP.is_le)
-        ts(["AC"], ["N1"], T.SC[:, 1:2], T.SC[:, 0:1], -0.5, OP.mult, 128.0, OP.add)
-        ts(["ON", "F1"], ["FB"], T.FB[:, 0:32], T.ON[:, 0:32], T.SC[:, 2:3], OP.mult)
-        ts(["AC", "N1"], ["NF"], T.SC[:, 3:4], T.SC[:, 0:1], 64.0, OP.is_gt, T.SC[:, 1:2], OP.mult)
-        act(["ON", "NF"], ["FBb"], T.FB[:, 32:64], T.ON[:, 0:32], AF.Copy, 0.0, T.SC[:, 3:4])
-        turn(["FB", "FBb"], ["FX"], T.FB[:, 64:128], T.FB[:, 0:64])
+        ts(["ON", "F1"], ["FB"], T.FB[:, 0:32], T.ON[:, 0:32], T.SC[:, 2:3], OP.mult, -15.5 / 16, OP.add)
+        turn(["FB"], ["FX"], T.FB[:, 64:96], T.FB[:, 0:32])
         emit("V", ["FX"], ["SF"], lambda e: e.tensor_reduce(T.SC[:, 4:5], T.FB[:, 64:80], AxisListType.X, OP.add))
-        emit("V", ["FX"], ["NP"], lambda e: e.tensor_reduce(T.SC[:, 5:6], T.FB[:, 96:112], AxisListType.X, OP.max))
-        ts(["TO", "SF"], ["EQM"], T.EQM[:], T.TO[:], T.SC[:, 4:5], OP.add, 16.0, OP.is_equal)
-        scan(["EQM", "ZR"], ["CU"], T.CU[:], T.EQM[:], T.ON[:, 32:288], 0.0, OP.add, OP.max)
-        ts(["CU", "NP"], ["OV"], T.OV[:], T.CU[:], T.SC[:, 5:6], OP.add, float(KEEP), OP.is_gt)
+        act(["TO", "SF"], ["AJ1", "NP"], T.AJ[:, 256:512], T.TO[:], AF.Sign, T.SC[:, 4:5], 1.0, T.SC[:, 5:6])
+        ts(["TO", "SF"], ["EQM"], T.EQM[:], T.TO[:], T.SC[:, 4:5], OP.add, 0.5, OP.is_equal)
+        scan(["EQM", "ZR"], ["CU"], T.CU[:], T.EQM[:], T.ON[:, 32:288], 32.0, OP.add, OP.max)
+        ts(["CU", "NP"], ["OV"], T.OV[:], T.CU[:], 2.0, OP.mult, T.SC[:, 5:6], OP.is_gt)
         tt(["TO", "OV"], ["Zx"], T.Z2[:], T.TO[:], T.OV[:], OP.add)
-        ts(["Zx", "SF"], ["GN"], T.GN[:], T.Z2[:], T.SC[:, 4:5], OP.add, 16.0, OP.is_le)
+        ts(["Zx", "SF"], ["GN"], T.GN[:], T.Z2[:], T.SC[:, 4:5], OP.add, 0.5, OP.is_le)
         scan(["GN", "ZR"], ["GS"], T.GS[:], T.GN[:], T.ON[:, 32:288], 255.0, OP.add, OP.max)
         scan(["GS", "GN"], ["M1"], T.M1[:], T.GS[:], T.GN[:], 0.0, OP.max, OP.mult)
         tt(["M1", "ID"], ["Y0"], T.Y0[:], T.M1[:], T.ID[:], OP.max)
-        scan(["EX", "Y0"], ["NSx"], T.NS[:], T.EX[:], T.Y0[:], 0.0, OP.add, OP.max)
-        ts(["NSx", "xq"], ["NI16"], T.NI16[:], T.NS[:, E15], T.PF[:, 5:6], OP.subtract)
-        act(["NSx", "nxq"], ["NS"], T.CL[:, 32:48], T.NS[:, E15], AF.Identity, T.PF[:, 14:15])
+        scan(["EX", "M1"], ["NSx"], T.NS[:], T.EX[:], T.M1[:], 0.0, OP.add, OP.max)
+        tt(["NSx", "CP"], ["NSw"], T.W3[:, 0:16], T.NS[:, E15], T.W3[:, 16:32], OP.max)
+        ts(["NSw", "xq"], ["NI16"], T.NI16[:], T.W3[:, 0:16], T.PF[:, 5:6], OP.subtract)
+        act(["NSw", "nxq"], ["NS"], T.CL[:, 32:48], T.W3[:, 0:16], AF.Identity, T.PF[:, 14:15])
         for b in range(4):
             k = PS[b]
             mm(["L%d" % t, "pad", "W"], k, 128, "W", 128 * b, "L", lo, True, False)
@@ -578,10 +575,10 @@ def rank_program(g, core, T, topo):
             T.cX[:, 256 * t + 256:256 * t + 512].bitcast(dt.uint32), T.cP[:, :].bitcast(dt.uint32).indirect(T.NI16[:])))
         emit("A", ["P", "Pb", "NI16"], [XN + "s"], lambda e, t=t: e.activation(
             T.sX[:, 256 * t + 256:256 * t + 512], T.sP[:, :].indirect(T.NI16[:]), AF.Copy))
-        ts(["NS"], ["GW"], T.SM[:, 0:16], T.CL[:, 32:48], 256.0, OP.is_ge)
-        ts(["NS"], ["GW2"], T.SM[:, 16:32], T.CL[:, 32:48], 256.0, OP.is_ge)
+        act(["NSw", "nxq"], ["NS2"], T.CL[:, 48:64], T.W3[:, 0:16], AF.Identity, T.PF[:, 14:15])
+        ts(["NS", "NS2"], ["GW"], T.SM[:, 0:32], T.CL[:, 32:64], 256.0, OP.is_ge)
         tt(["NS", "LW", "CL"], ["D1"], T.SM[:, 32:64], T.CL[:, 16:48], T.CL[:, 0:32], OP.subtract)
-        tt(["GW", "GW2", "D1"], ["D2"], T.SM[:, 64:96], T.SM[:, 0:32], T.SM[:, 32:64], OP.mult)
+        tt(["GW", "D1"], ["D2"], T.SM[:, 64:96], T.SM[:, 0:32], T.SM[:, 32:64], OP.mult)
         tt(["D2", "LW", "CL"], ["D3"], T.SM[:, 96:128], T.SM[:, 64:96], T.CL[:, 0:32], OP.add)
         cp(["D3"], ["M16"], T.M16[:], T.SM[:, 96:128])
 

import numpy as np
from concourse.bass import DstId, RemoteDMATransfer
from concourse.mybir import dt, AluOpType, AxisListType, ActivationFunctionType

OP = AluOpType
AF = ActivationFunctionType
ROUNDS, KEEP = 3, 96
F, B, I, U, X4, U8 = "float32", "bfloat16", "int32", "uint16", "float8_e4m3fn_x4", "uint8"

SCRATCH = {}


def _sb(dtype, **widths):
    for name in widths:
        SCRATCH[name] = ("sbuf", [128, widths[name]], dtype)


def _q(**widths):
    for name in widths:
        SCRATCH["c" + name] = ("sbuf", [128, widths[name]], X4)
        SCRATCH["s" + name] = ("sbuf", [128, widths[name]], U8)


_sb(B, XT=1024, UT=512, VTL=512)
_sb(I, OL=16, PC=1, PI=4, OI=72, RI=32, CI=24, LI=144)
_q(W=512, U=128, UP=384, V=128, X=1024, L=320, P=384, E=384)
_q(K=1024)
_q(C=1664)
_sb(B, TK=5120)
_sb(F, IR=256, ID=256, TI=128, BK=512, PF=16, RQ=256, BS=256, BE=256, TR=128, CY=368, CB=368, CW=16, CX=16, CT=16)
_sb(U, OU=72)
_sb(B, ME=256, KP=256, ON=288, EX=256)
_sb(F, MS=512, SWS=256, SG=256, SWE=256, EG=256, SB2=2, DL=4, TH0=128, TH1=128)
_sb(B, BT=1024, CT2=8192, AJ=1024)
_sb(F, VH=1792, VT=1792, T6=80, CM=96, XX=192, MN=80, T1=32)
_sb(B, FT=1024, FU=1024, Z=1024, ET=512, RT=512)
_sb(F, AR=32, RW=32, EC=256, EP=48, EF=256, PK=96)
_sb(U, EP16=16, EO=32, LS=144, LL=144, R16=16, NI16=16, M16=32, L16=16)
_sb(B, RD=512, XR=512, RX=512)
_sb(F, XE=256, ES=96, RS=256)
_sb(F, CA=8, CJ=512, CF=16, QQ=176, W3=32)
_sb(B, RP=256, TO=256, FB=128, EQM=256, CU=256, OV=256, Z2=256, GN=256)
_sb(F, SC=16, GS=256, M1=256, Y0=256, NS=256, SM=208, YA=256, YB=256, YX=352, NR=256, CL=64, YO=256)
for _i in range(8):
    SCRATCH["P%d" % _i] = ("psum", [128, 512], F)
PS = ["P%d" % i for i in range(8)]
PLACE = {"B": ("C", 0)}
TILE_N = (128, 128, 192, 256)
for _i in range(4):
    PLACE["X%d" % _i] = ("X", 256 * _i)
    PLACE["KR%d" % _i] = ("K", 128 * _i)
    PLACE["C%d" % _i] = ("C", 256 + sum(TILE_N[:_i]))
    PLACE["D%d" % _i] = ("C", 960 + sum(TILE_N[:_i]))
for _i in range(3):
    PLACE["E%d" % _i] = ("E", 128 * _i)
for _i, _k in enumerate(("KS", "KB", "KT", "KU")):
    PLACE[_k] = ("K", 512 + 128 * _i)
WAKE, SLACK, FLIGHT = 0.3, 0.25, 4.5
LONG = {"MS": .25, "MSE": .25, "SWS": .25, "SWE": .25, "SG": .25, "EG": .25, "V0": .25, "TT": .25, "VT": .25, "XE": .25,
        "EC": .25, "RS": .25, "NSx": .25, "GS": .25, "NRx": .25, "BTe": .37, "BTf": .37, "Z": .37, "BTa": .13, "BTb": .13,
        "BTc": .13, "BTd": .13, "EF": .8, "XS": .13, "RY": .13, "TO": .13, "EQM": .13, "CU": .13, "OV": .13, "GN": .13,
        "Zx": .45, "Y0": .45, "RD": .13, "FU": .45, "X": .36, "Xs": .36, "VH": .37, "CJ": .39, "CA": .39, "FT": .23,
        "XR": .36, "RX": .36, "ET": .2, "RP": .36, "YA": .36, "YB": .36, "YX": .36, "M": .3, "TH": .13, "AC": .25,
        "P": .24, "Pb": .13, "B": .24, "C": .17, "D": .17, "E": .13, "RT": .1, "TKS": .45, "TKB": 1.2, "TKT": 1.2, "TK": 1.2,
        "IR": .6, "ID": .6, "BK": 1.0, "CY": .8, "RQ": .23, "ME": .23, "KP": .23, "BS": .23, "BE": .23, "EX": .3, "CB": .3}


def duration(q, key):
    if q == "P":
        return 0.2
    if q == "G" and key[:3] == "snd":
        return 0.7
    if key[:2] == "ct" or key[:2] == "AR" and "." in key:
        return 0.02 + 0.00083 * max(64, 16 * int(key.split(".")[1]))
    return LONG.get(key.rstrip("0123456789s") or key, LONG.get(key.rstrip("0123456789"), 0.075))

SEMAPHORES = ["sV", "sA", "sP", "sG", "dX", "dU", "dO", "dW", "dVV", "dPad", "dY", "dLk", "dOc", "ls",
              "aC0", "aC1", "aC2", "aL0", "aL1", "aL2"]


def rank_program(g, core, T, topo):
    rank = T.rank_of(core)
    if rank is None:
        return
    cores = T.cores
    n_ranks = len(cores)
    nxt, prv = cores[(rank + 1) % n_ranks], cores[(rank - 1) % n_ranks]
    eng = {"V": g.vector, "A": g.scalar, "P": g.tensor, "G": g, "S": g.sync}
    own = {"V": "sV", "A": "sA", "P": "sP", "G": "sG"}
    cnt, known, lastw, readers = {}, {q: {} for q in eng}, {}, {}

    def sync(q, toks):
        for s, n, clk in sorted(toks, key=lambda t: -sum(t[2].values())):
            if known[q].get(s, 0) < n:
                eng[q].wait_ge(T.sem[s], n)
                for k in clk:
                    known[q][k] = max(known[q].get(k, 0), clk[k])
                known[q][s] = max(known[q].get(s, 0), n)

    def deps(q, r, w):
        toks, me = [], own.get(q)
        for k in r:
            if k in lastw and not (q == "P" and lastw[k][0] == "sP"):
                toks.append(lastw[k])
            if k in PS:
                toks += [t for s, t in readers.get(k, {}).items() if s != me]
        for k in w:
            if k in lastw and not (q == "P" and lastw[k][0] == "sP"):
                toks.append(lastw[k])
            toks += [t for s, t in readers.get(k, {}).items()]
        sync(q, toks)

    def done(tok, r, w):
        for k in r:
            readers.setdefault(k, {})[tok[0]] = tok
        for k in w:
            lastw[k] = tok
            readers[k] = {}

    nodes = []

    def emit(q, r, w, fn):
        def issue():
            deps(q, r, w)
            s = own[q]
            fn(eng[q]).then_inc(T.sem[s], 1)
            cnt[s] = cnt.get(s, 0) + 1
            clk = dict(known[q])
            clk[s] = cnt[s]
            done((s, cnt[s], clk), r, w)
        nodes.append((q, r, w, issue, duration(q, w[0]), 0.0))

    def dma(q, s, r, w, pairs):
        def issue():
            deps(q, r, w)
            for o, i in pairs:
                eng[q].dma_start(o, i).then_inc(T.sem[s], 16)
                cnt[s] = cnt.get(s, 0) + 16
            done((s, cnt[s], dict(known[q])), r, w)
        nodes.append((q, r, w, issue, 0.1, 2.0))

    def arrival(key, r, tok):
        nodes.append(("R", r, [key], lambda: done(tok, [], [key]), 0.0, FLIGHT))

    def schedule():
        n = len(nodes)
        succ, left = [[] for _ in range(n)], [0] * n
        wr, rd = {}, {}

        def edge(a, b, lag):
            if a != b:
                succ[a].append((b, lag))
                left[b] += 1
        for i, (q, r, w, fn, c, late) in enumerate(nodes):
            for k in r:
                if k in wr:
                    edge(wr[k], i, 0.0 if q == "P" and nodes[wr[k]][0] == "P" else WAKE)
                if k in PS:
                    for j in rd.get(k, []):
                        if nodes[j][0] != q:
                            edge(j, i, WAKE)
            for k in w:
                if k in wr:
                    edge(wr[k], i, 0.0 if q == "P" and nodes[wr[k]][0] == "P" else WAKE)
                for j in rd.get(k, []):
                    edge(j, i, WAKE)
            for k in r:
                rd.setdefault(k, []).append(i)
            for k in w:
                wr[k], rd[k] = i, []
        rest = [0.0] * n
        for i in range(n - 1, -1, -1):
            rest[i] = nodes[i][4] + nodes[i][5] + max([lag + rest[j] for j, lag in succ[i]] + [0.0])
        ready, free, todo = [0.0] * n, {}, [i for i in range(n) if not left[i]]
        while todo:
            best = None
            for i in todo:
                at = max(ready[i], free.get(nodes[i][0], 0.0))
                if best is None or (at, -rest[i]) < best[:2]:
                    best = (at, -rest[i], i)
            at, i = best[0], best[2]
            for j in todo:
                if nodes[j][0] == nodes[i][0] and max(ready[j], free.get(nodes[j][0], 0.0)) <= at + SLACK and rest[j] > rest[i]:
                    i = j
            at = max(ready[i], free.get(nodes[i][0], 0.0))
            todo.remove(i)
            nodes[i][3]()
            end = at + nodes[i][4]
            free[nodes[i][0]] = end
            for j, lag in succ[i]:
                ready[j] = max(ready[j], (at if lag == 0.0 and nodes[j][0] == nodes[i][0] else end + nodes[i][5]) + lag)
                left[j] -= 1
                if not left[j]:
                    todo.append(j)

    def tt(r, w, out, a, b, op):
        emit("V", r, w, lambda e: e.tensor_tensor(out, a, b, op))

    def ts(r, w, out, a, s1, o1, s2=None, o2=None):
        if o2 is None:
            emit("V", r, w, lambda e: e.tensor_scalar(out, a, s1, None, o1))
        else:
            emit("V", r, w, lambda e: e.tensor_scalar(out, a, s1, s2, o1, o2))

    def cp(r, w, out, a):
        emit("V", r, w, lambda e: e.tensor_copy(out, a))

    def scan(r, w, out, d0, d1, init=0.0, o0=OP.mult, o1=OP.add):
        emit("V", r, w, lambda e: e.tensor_tensor_scan(out, d0, d1, init, o0, o1))

    def turn(r, w, out, a):
        emit("V", r, w, lambda e: e.transpose(out, a))

    def fill(w, ap, x):
        emit("V", [], w, lambda e: e.memset(ap, x))

    def quant(r, name, c0, c1, tile):
        k, o = PLACE.get(name, (name, 0))
        emit("V", r, [name if c0 == 0 else name + "b"],
             lambda e: e.quantize_mx(T["c" + k][:, o + c0:o + c1], T["s" + k][:, o + c0:o + c1], tile))

    def act(r, w, out, a, fn=AF.Copy, bias=0.0, scale=1.0, acc=None):
        if acc is None:
            emit("A", r, w, lambda e: e.activation(out, a, fn, bias, scale))
        else:
            emit("A", r, w, lambda e: e.activation(out, a, fn, bias, scale, accum_out=acc))

    def mm(r, bank, n, L, l0, R, r0, start=True, stop=True):
        L, lo_ = PLACE.get(L, (L, 0))
        R, ro_ = PLACE.get(R, (R, 0))
        l0, r0 = l0 + lo_, r0 + ro_
        emit("P", r, [bank], lambda e: e.matmul_mx(
            T[bank][:, 0:n], T["c" + L][:, l0:l0 + 128], T["s" + L][:, l0:l0 + 128],
            T["c" + R][:, r0:r0 + n], T["s" + R][:, r0:r0 + n], start, stop))

    def iota(w, out, pattern, base, cm):
        emit("G", [], w, lambda e: e.iota(out, pattern, base, cm, allow_small_or_imprecise_dtypes=True))

    def iotai(w, out, pattern, base, cm):
        emit("G", [], w, lambda e: e.iota(out, pattern, base, cm))

    dma("S", "dX", [], ["XT"], [(T.XT[:], T.x[:])])
    dma("A", "dU", [], ["UT"], [(T.UT[:], T.u[:])])
    dma("S", "dO", [], ["OL"], [(T.OL[:], T.ol[:])])
    dma("A", "dW", [], ["W"], [(T.cW[:].bitcast(dt.uint8), T.wc[:]), (T.sW[:], T.ws[:])])
    dma("S", "dVV", [], ["VTL"], [(T.VTL[:], T.v[:])])

    iotai(["PC"], T.PC[:], [[0, 1]], 0, 1)
    iotai(["OI"], T.OI[:, 0:8], [[16, 8]], 0, 0)
    iotai(["OI"], T.OI[:, 8:16], [[16, 8]], 1, 0)
    iotai(["OI"], T.OI[:, 16:24], [[0, 8]], 8, 0)
    iotai(["OI"], T.OI[:, 24:40], [[1, 16]], 0, 0)
    iotai(["OI"], T.OI[:, 40:56], [[16, 16]], 15, 0)
    iotai(["OI2"], T.OI[:, 56:72], [[2, 8], [0, 2]], 0, 0)
    iota(["IR"], T.IR[:], [[0, 16], [1, 16]], 0, 0)
    iota(["TI"], T.TI[:], [[1, 128]], 0, -1)
    iota(["ID"], T.ID[:], [[1, 256]], 0, 0)
    iota(["BK"], T.BK[:], [[1, 8], [0, 64]], 0, 0)
    iota(["CW"], T.CW[:], [[16, 16]], 0, 0)
    iota(["CT0"], T.CT[:], [[32, 8], [0, 2]], 0, 0)
    iota(["CY"], T.CY[:], [[1, 368]], -112, 0)
    iota(["T128"], T.TK[:, 4096:4608], [[0, 512]], 128, 0)
    fill(["T256"], T.TK[:, 4608:5120], 256.0)
    cp(["OI"], ["OU"], T.OU[:, 0:56], T.OI[:, 0:56])
    ts(["PC"], ["PI"], T.PI[:, 0:1], T.PC[:], 15, OP.bitwise_and)
    ts(["PC"], ["PI1"], T.PI[:, 1:2], T.PC[:], 4, OP.arith_shift_right)
    ts(["PI1"], ["PI2"], T.PI[:, 2:3], T.PI[:, 1:2], 1, OP.bitwise_and)
    cp(["PI"], ["q"], T.PF[:, 0:1], T.PI[:, 0:1])
    cp(["PI1"], ["g"], T.PF[:, 1:2], T.PI[:, 1:2])
    cp(["PI2"], ["m1"], T.PF[:, 2:3], T.PI[:, 2:3])
    ts(["OI2", "m1"], ["OU2"], T.OU[:, 56:72], T.OI[:, 56:72], T.PF[:, 2:3], OP.add)
    ts(["q"], ["qn"], T.PF[:, 4:5], T.PF[:, 0:1], -1.0, OP.mult, -0.5, OP.add)
    ts(["BK", "g"], ["TKS"], T.TK[:, 2048:2560], T.BK[:], T.PF[:, 1:2], OP.is_equal)
    emit("G", ["T256"], ["TKB"], lambda e: e.affine_select(
        T.TK[:, 2560:3072], T.TK[:, 4608:5120], [[0, 128], [-1, 4]], OP.is_gt, 0.0, 2, 0))
    for i in (2, 3):
        emit("G", ["TKS"], ["TKT%d" % i], lambda e, i=i: e.affine_select(
            T.TK[:, 2048 + 512 * i:2560 + 512 * i], T.TK[:, 2048:2560], [[0, 128], [1, 4]], OP.is_equal, 0.0, -i, 0))
    for b in range(4):
        emit("G", ["T128"], ["TK%d" % b], lambda e, b=b: e.affine_select(
            T.TK[:, 512 * b:512 * b + 512], T.TK[:, 4096:4608], [[-1, 128], [1000, 4]], OP.is_equal, 0.0, -1000 * b, 1))
    ts(["q"], ["nq"], T.PF[:, 12:13], T.PF[:, 0:1], -1.0, OP.mult)
    act(["IR", "nq"], ["RQ"], T.RQ[:], T.IR[:], AF.Identity, T.PF[:, 12:13])
    act(["RQ"], ["BS"], T.BS[:], T.RQ[:], AF.Abs)
    act(["BS"], ["ME"], T.ME[:], T.BS[:], AF.Relu, 1.0, -1.0)
    act(["IR"], ["KP"], T.KP[:], T.IR[:], AF.Sign)
    act(["RQ"], ["BE"], T.BE[:], T.RQ[:], AF.Sign, 0.5)
    act(["BE"], ["BE"], T.BE[:], T.BE[:], AF.Relu)
    act(["BE"], ["BS"], T.BS[:], T.BE[:], AF.Copy, 0.0, -2.0 ** 90)
    act(["BE"], ["RQ"], T.RQ[:], T.BE[:], AF.Copy, 0.0, 512.0)
    act(["ME"], ["EX"], T.EX[:], T.ME[:], AF.Copy, 0.0, -2.0 ** 20)
    tt(["RQ", "EX"], ["EX"], T.EX[:], T.RQ[:], T.EX[:], OP.add)
    act(["BE"], ["BE"], T.BE[:], T.BE[:], AF.Copy, 0.0, 2.0 ** 90)
    act(["TI"], ["TR"], T.TR[:], T.TI[:], AF.Sign, 0.5, -1.0)
    act(["TR"], ["TR"], T.TR[:], T.TR[:], AF.Relu)
    ts(["q"], ["xq"], T.PF[:, 5:6], T.PF[:, 0:1], -512.0, OP.mult, 7680.0, OP.add)
    ts(["xq"], ["nxq"], T.PF[:, 14:15], T.PF[:, 5:6], -1.0, OP.mult)
    for i in range(4):
        ts(["xq"], ["xq4"], T.PF[:, 8 + i:9 + i], T.PF[:, 5:6], -4.0, OP.mult, float(i), OP.add)
    quant(["UT"], "U", 0, 128, T.UT[:, 0:512])
    emit("V", ["U", "OU"], ["UPc"], lambda e: e.tensor_copy(
        T.cUP[:, 0:384].bitcast(dt.uint32), T.cU[:, 0:128].bitcast(dt.uint32).indirect(T.OU[:, 0:24])))
    emit("A", ["U", "OU"], ["UPs"], lambda e: e.activation(
        T.sUP[:, 0:384], T.sU[:, 0:128].indirect(T.OU[:, 0:24]), AF.Copy))
    UPK = ["UPc", "UPs"]
    quant(["XT"], "X0", 0, 256, T.XT[:])
    for a in range(4):
        o, e = 1024 * a + 256 * a, 1024 * a + 4 * TILE_N[a]
        fill(["CT2%d" % a], T.CT2[:, o:e], 0.0)
        act(["CT2%d" % a], ["CT3%d" % a], T.CT2[:, 4096 + o:4096 + e], T.CT2[:, o:e])
    fill(["AR"], T.AR[:], 0.0)
    dma("S", "dPad", ["X0"], ["pad"], [(T.cL[:, 288:320].bitcast(dt.uint8), T.cX[:, 0:32].bitcast(dt.uint8)),
                                       (T.sL[:, 288:320], T.sX[:, 0:32])])

    ZC = ["CT%d%d" % (i, a) for i in (2, 3) for a in range(4)]

    def late_constants():
        for b in range(4):
            quant(["TK%d" % b], "KR%d" % b, 0, 128, T.TK[:, 512 * b:512 * b + 512])

    def birth_constants():
        for i, k in enumerate(("KS", "KB", "KT", "KU")):
            quant(["TKS", "TKB", "TKT2", "TKT3"], k, 0, 128, T.TK[:, 2048 + 512 * i:2560 + 512 * i])
        ts(["CW", "xq"], ["CX"], T.CX[:], T.CW[:], T.PF[:, 5:6], OP.subtract)
        ts(["CW", "xq"], ["CP"], T.W3[:, 16:32], T.CW[:], T.PF[:, 5:6], OP.add)
        ts(["PC"], ["PI3"], T.PI[:, 3:4], T.PC[:], 31, OP.bitwise_and)
        cp(["PI3"], ["x32"], T.PF[:, 6:7], T.PI[:, 3:4])
        ts(["x32", "xq"], ["x32q"], T.PF[:, 7:8], T.PF[:, 6:7], T.PF[:, 5:6], OP.add)
        ts(["CT0", "x32q"], ["CT"], T.CT[:], T.CT[:], T.PF[:, 7:8], OP.add)

    def count_constants():
        ts(["nq"], ["nq128"], T.PF[:, 13:14], T.PF[:, 12:13], -128.0, OP.add)
        act(["CY", "nq128"], ["CB"], T.CB[:], T.CY[:], AF.Abs, T.PF[:, 13:14])
        act(["CB"], ["CB"], T.CB[:], T.CB[:], AF.Relu, 512.0, -512.0)
        act(["CY", "nq"], ["CY"], T.CY[:], T.CY[:], AF.Abs, T.PF[:, 12:13])
        act(["CY"], ["CY"], T.CY[:], T.CY[:], AF.Relu, 1.0, -1.0)
        tt(["CY", "CB"], ["CB"], T.CB[:], T.CB[:], T.CY[:], OP.add)
        fill(["ON"], T.ON[:, 0:32], 1.0)
        fill(["ZR"], T.ON[:, 32:288], 0.0)
        fill(["CM6"], T.CM[:], 0.0)
        fill(["Q4z"], T.QQ[:, 48:80], 0.0)
        fill(["ETz"], T.ET[:, 384:512], 0.0)
        fill(["RTz"], T.RT[:, 384:512], 0.0)
        quant(["VTL"], "V", 0, 128, T.VTL[:])

    ts(["CW", "q"], ["CW"], T.CW[:], T.CW[:], T.PF[:, 0:1], OP.add)
    cp(["CW"], ["CL"], T.CL[:, 0:16], T.CW[:])
    cp(["OL"], ["LW"], T.CL[:, 16:32], T.OL[:])
    cp(["OL"], ["L16"], T.L16[:], T.OL[:])

    BC, BC15, BC32 = T.OU[:, 24:40], T.OU[:, 40:56], T.OU[:, 56:72]
    E15 = slice(15, 256, 16)
    rid, pid = topo.addr(nxt)[0], topo.addr(nxt)[1]
    mask = topo.mask(core, nxt)
    n_eng = len(topo.engines(core, nxt))
    n_arr = len(topo.engines(prv, core))
    sent = [0]

    def send(r, out, src, rsem):
        def issue():
            deps("G", r, [])
            g.remote_dma(out, src, T.sem[rsem], T.sem.ls, pid, rid, mask)
            sent[0] += n_eng
        nodes.append(("G", r, ["snd" + rsem], issue, 0.7, 0.0))

    pending = []

    for t in range(ROUNDS):
        X = "X%d" % t
        XK = [X, X + "s"]
        mm(XK + UPK, "P7", 256, "UP", 0, X, 0)
        mm(XK + UPK, "P5", 128, X, 0, "UP", 256)
        mm(XK + UPK, "P6", 128, X, 128, "UP", 256)
        mm(XK + UPK, "P4", 256, "UP", 256, X, 0)
        mm(XK + UPK, "P3", 256, "UP", 128, X, 0)
        act(["P5"], ["SB0"], T.SB2[:, 0:1], T.P5[:, 0:1])
        act(["P6"], ["SB1"], T.SB2[:, 1:2], T.P6[:, 0:1])
        act(["SB0", "SB1"], ["DL"], T.DL[:, 0:2], T.SB2[:, 0:2], AF.Abs, 0.0, 1.25 * 2.0 ** -24)
        tt(["P7", "ME"], ["MS"], T.MS[:, 0:256], T.P7[:, 0:256], T.ME[:], OP.mult)
        if t == 0:
            birth_constants()
        act(["DL"], ["DL2"], T.DL[:, 2:4], T.DL[:, 0:2], AF.Identity, 2.0 ** -120)
        for h in range(2):
            act(["TR", "DL2", "SB0", "SB1"], ["TH%d" % h], T["TH%d" % h][:], T.TR[:], AF.Identity,
                T.SB2[:, h:h + 1], T.DL[:, 2 + h:3 + h])
        for f in pending[:2]:
            f()
        scan(["KP", "MS"], ["SWS"], T.SWS[:], T.KP[:], T.MS[:, 0:256])
        tt(["P7", "BS"], ["SG"], T.SG[:], T.P7[:, 0:256], T.BS[:], OP.add)
        ts(["P4", "SB0"], ["BTa"], T.BT[:, 512:1024:4], T.P4[:, 128:256], T.SB2[:, 0:1], OP.is_ge)
        ts(["P4", "SB1"], ["BTb"], T.BT[:, 1:512:4], T.P4[:, 0:128], T.SB2[:, 1:2], OP.is_gt)
        tt(["P3", "ME"], ["MSE"], T.MS[:, 256:512], T.P3[:, 0:256], T.ME[:], OP.mult)
        tt(["SWS", "SG", "OU"], ["BTe"], T.BT[:, 2:1024:4], T.SWS[:].indirect(BC15), T.SG[:], OP.is_lt)
        scan(["KP", "MSE"], ["SWE"], T.SWE[:], T.KP[:], T.MS[:, 256:512])
        tt(["P3", "BE"], ["EG"], T.EG[:], T.P3[:, 0:256], T.BE[:], OP.add)
        tt(["P4", "TH0"], ["BTc"], T.BT[:, 0:512:4], T.P4[:, 0:128], T.TH0[:], OP.is_ge)
        tt(["P4", "TH1"], ["BTd"], T.BT[:, 513:1024:4], T.P4[:, 128:256], T.TH1[:], OP.is_ge)

        tt(["SWE", "EG", "OU"], ["BTf"], T.BT[:, 3:1024:4], T.SWE[:].indirect(BC15), T.EG[:], OP.is_gt)

        def pair(s, m):
            bank, w, k, op = (("P7", T.SWS, "SWS", OP.is_gt), ("P3", T.SWE, "SWE", OP.is_lt))[s]
            if m:
                o, n = 4096 * s + 1024 * (m // 4), 64 * m
                v = T.CT2[:, o + m % 4:o + n:4]
                ts([bank, k] + ZC, ["ct%d.%d" % (s, m)], v, T[bank][:, 0:16 * m], w[:, 16 * m + 15:16 * m + 16], op)
                j = m % 4
                act(["ct%d.%d" % (s, m), "AR"], ["AR%d.%d" % (s, m), "AJ%d" % j], T.AJ[:, 256 * j:256 * j + 16 * m], v,
                    AF.Copy, 0.0, 1.0, T.AR[:, 16 * s + m:16 * s + m + 1])

        def pair_sum(s, a):
            o, n, k, bank = 4096 * s + 1024 * a, TILE_N[a], "CD"[s] + str(a), ("P4", "P5")[s]
            quant(["ct%d.%d" % (s, m) for m in range(4 * a, 4 * a + 4) if m] + ZC, k, 0, n, T.CT2[:, o:o + 4 * n])
            mm([k, "KS"], bank, n, "KS", 0, k, 0, False, a == 3)

        def row_sum(s):
            scan(["KP", ("BTe", "BTf")[s]], ["RD%d" % s], T.RD[:, 256 * s:256 * s + 256], T.KP[:], T.BT[:, 2 + s:1024:4])
            tt(["RD%d" % s, "AR"] + ["AR%d.%d" % (s, m) for m in range(1, 16)], ["RW%d" % s], T.RW[:, 16 * s:16 * s + 16],
               T.RD[:, 256 * s + 15:256 * s + 256:16], T.AR[:, 16 * s:16 * s + 16], OP.add)

        pair(0, 15)
        quant(["BTa", "BTb", "BTc", "BTd", "BTe", "BTf"], "B", 0, 256, T.BT[:])
        mm(["B", "KB"], "P6", 256, "KB", 0, "B", 0)
        mm(["B", "KT"], "P4", 256, "KT", 0, "B", 0, True, False)
        if t == 0:
            late_constants()
        for b in range(4):
            mm(XK + ["KR%d" % b], ("P0", "P1", "P2", "P5")[b], 256, "KR%d" % b, 0, X, 0)
        pair(0, 14)
        tt(["P6", "ID"], ["V0"], T.VH[:, 1536:1792], T.P6[:, 0:256], T.ID[:], OP.add)
        pair(0, 13)
        pair(0, 12)
        for m in range(11, 3, -1):
            pair(0, m)
        for f in pending[2:]:
            f()
        for m in range(3, 0, -1):
            pair(0, m)
        for a in range(4):
            pair_sum(0, a)
        if t == 0:
            count_constants()
        for i in range(6):
            src, k = (T.VH[:, 1536:1792], "V0") if i == 0 else (T.VH[:, 256 * i - 256:256 * i], "VH%d" % (i - 1))
            act([k, "L16"], ["VH%d" % i], T.VH[:, 256 * i:256 * i + 256], src.indirect(T.L16[:]),
                AF.Identity, 65536.0)
            if i == 0:
                row_sum(0)
                act(["RW0", "OU"], ["XR"], T.XR[:, 0:256], T.RW[:, 0:16].indirect(BC))
        def half(b):
            k = ("P0", "P1", "P2", "P5")[b]
            act([k], ["FT%d" % b], T.FT[:, 256 * b:256 * b + 256], T[k][:, 0:256], AF.Copy, 0.0, 2.0 ** -8)
            act([k], ["FU%d" % b], T.FU[:, 256 * b:256 * b + 256], T[k][:, 0:256], AF.Copy, 0.0, 2.0 ** -8)
        half(3)
        mm(["B", "KU"], "P5", 256, "KU", 0, "B", 0, True, False)
        for m in range(15, 7, -1):
            pair(1, m)
        turn(["XR"], ["XS"], T.XR[:, 256:512], T.XR[:, 0:256])
        turn(["P4"], ["TT"], T.VT[:, 1536:1792], T.P4[:, 0:256])
        scan(["EX", "XS"], ["XE"], T.XE[:], T.EX[:], T.XR[:, 256:512], 0.0, OP.add, OP.max)
        for m in range(7, 0, -1):
            pair(1, m)
            if m == 6:
                tt(["TT", "CT"], ["T1a"], T.T1[:, 0:16], T.VT[:, 1536:1792:16], T.CT[:], OP.add)
            if m == 4:
                tt(["T1a", "XE"], ["T1b"], T.T1[:, 16:32], T.T1[:, 0:16], T.XE[:, E15], OP.subtract)
                for i in range(5):
                    act(["T1b"], ["T6%d" % i], T.T6[:, 16 * i:16 * i + 16], T.T1[:, 16:32], AF.Identity,
                        255.5 + 65536.0 * (i + 1), 256.0)
        for b in range(3):
            half(b)
        for a in range(4):
            pair_sum(1, a)
        for i in range(6):
            turn(["VH%d" % i], ["VT%d" % i], T.VT[:, 256 * i:256 * i + 256], T.VH[:, 256 * i:256 * i + 256])
        VTK = ["VT%d" % i for i in range(6)]
        tt(VTK[:5] + ["T6%d" % i for i in range(5)] + ["CM6"], ["CM"], T.CM[:, 0:80], T.VT[:, 0:1280:16], T.T6[:], OP.is_gt)
        act(["CM", "CM6"], ["XXa"], T.XX[:, 0:96], T.CM[:], AF.Copy, 0.0, 2.0 ** 20)
        tt(["XXa"] + VTK, ["XXb"], T.XX[:, 96:192], T.XX[:, 0:96], T.VT[:, 0:1536:16], OP.add)
        tt(["XXb"], ["MNa"], T.MN[:, 0:48], T.XX[:, 96:144], T.XX[:, 144:192], OP.min)
        tt(["MNa"], ["MNb"], T.MN[:, 48:64], T.MN[:, 0:16], T.MN[:, 16:32], OP.min)
        tt(["MNa", "MNb"], ["RI0"], T.RI[:, 0:16], T.MN[:, 48:64], T.MN[:, 32:48], OP.min)
        ts(["RI0"], ["RI1"], T.RI[:, 16:32], T.RI[:, 0:16], 255, OP.bitwise_and)
        cp(["RI1"], ["RI2"], T.EP[:, 32:48], T.RI[:, 16:32])
        act(["RI2", "OU"], ["RX"], T.RX[:, 0:256], T.EP[:, 32:48].indirect(BC))
        row_sum(1)
        turn(["RX"], ["RY"], T.RX[:, 256:512], T.RX[:, 0:256])
        scan(["EX", "RY"], ["RS"], T.RS[:], T.EX[:], T.RX[:, 256:512], 0.0, OP.add, OP.max)
        ts(["RS", "xq"], ["R16"], T.R16[:], T.RS[:, E15], T.PF[:, 5:6], OP.subtract)
        for z in range(8):
            act(["CB", "R16"], ["CJ%d" % (z % 2), "CA%d" % z], T.CJ[:, 256 * (z % 2):256 * (z % 2) + 256], T.CB[:, 112 - 16 * z:368 - 16 * z].indirect(T.R16[:]),
                AF.Copy, 0.0, 1.0, T.CA[:, z:z + 1])
        scan(["EX", "P5"], ["EC"], T.EC[:], T.EX[:], T.P5[:, 0:256], 0.0, OP.add, OP.max)
        tt(["CX", "RW1"], ["EPa"], T.EP[:, 0:16], T.CX[:], T.RW[:, 16:32], OP.subtract)
        tt(["EPa", "EC"], ["EP"], T.EP[:, 16:32], T.EP[:, 0:16], T.EC[:, E15], OP.add)
        cp(["EP"], ["EP16"], T.EP16[:], T.EP[:, 16:32])
        cp(["ID", "EP16"], ["EF"], T.EF[:, 0:256].indirect(T.EP16[:]), T.ID[:])
        for b in range(4):
            f = T.FT[:, 256 * b:256 * b + 256]
            tt(["FT%d" % b, "FU%d" % b, "R16"], ["Z%d" % b], T.Z[:, b:1024:4], f.indirect(T.R16[:]),
               T.FU[:, 256 * b:256 * b + 256], OP.add)
            if b == 1:
                scan(["EX", "EF"], ["ES"], T.ES[:], T.EX[:, 0:96], T.EF[:, 0:96], 0.0, OP.add, OP.max)
            if b == 2:
                for i in range(4):
                    ts(["ES", "xq4"], ["EO%d" % i], T.EO[:, 8 * i:8 * i + 6], T.ES[:, 15:96:16], 4.0, OP.mult,
                       T.PF[:, 8 + i:9 + i], OP.add)
        ZK = ["Z0", "Z1", "Z2", "Z3"]
        for b in range(4):
            (cp, cp, act, act)[b](ZK + ["EO%d" % b], ["ET%d" % b], T.ET[:, b:384:4], T.Z[:].indirect(T.EO[:, 8 * b:8 * b + 6]))
        act(["EF"], ["PKa"], T.PK[:, 0:48], T.EF[:, 48:96], AF.Copy, 0.0, 256.0)
        lo = KEEP * (ROUNDS - 1 - t)

        def send_columns():
            quant(["ET0", "ET1", "ET2", "ET3", "ETz"], "E%d" % t, 0, 128, T.ET[:])
            send(["E%d" % t], T.cL[:, lo:lo + KEEP].bitcast(dt.uint8),
                 T.cE[:, 128 * t:128 * t + KEEP].bitcast(dt.uint8), "aC%d" % t)
            send(["E%d" % t], T.sL[:, lo:lo + KEEP], T.sE[:, 128 * t:128 * t + KEEP], "aC%d" % t)
            send(["LS%d" % t], T.LL[:, 48 * t:48 * t + 48], T.LS[:, 48 * t:48 * t + 48], "aL%d" % t)
            arrival("L%d" % t, ["sndaC%d" % t], ("aC%d" % t, 2 * n_arr, {}))
            arrival("LL%d" % t, ["sndaL%d" % t], ("aL%d" % t, n_arr, {}))
        tt(["PKa", "EF"], ["PKb"], T.PK[:, 48:96], T.PK[:, 0:48], T.EF[:, 0:48], OP.add)
        quant(ZK, "P", 0, 256, T.Z[:])
        cp(["PKb"], ["LS%d" % t], T.LS[:, 48 * t:48 * t + 48], T.PK[:, 48:96])
        cp(["CA%d" % z for z in range(8)], ["CI0"], T.CI[:, 0:8], T.CA[:])
        ts(["CI0"], ["CI1"], T.CI[:, 8:16], T.CI[:, 0:8], 511, OP.bitwise_and)
        ts(["CI0"], ["CI2"], T.CI[:, 16:24], T.CI[:, 0:8], 9, OP.arith_shift_right)
        Q1, Q2, Q3, Q4, Q5, Q6, Q7 = [(a, a + 32) for a in (0, 16, 32, 48, 80, 112, 144)]

        def qq(q, a=0, b=32, step=1, p=0, np_=128):
            return T.QQ[p:p + np_, q[0] + a:q[0] + b:step]
        cp(["CI1", "CI2"], ["Q1"], qq(Q1, 0, 16, 1, 0, 64), T.CI[64:128, 8:24])
        cp(["CI1", "CI2"], ["Q1b"], qq(Q1, 0, 16, 1, 64, 64), T.CI[0:64, 8:24])
        tt(["CI1", "CI2", "Q1", "Q1b"], ["Q2"], qq(Q2, 0, 16), T.CI[:, 8:24], qq(Q1, 0, 16), OP.add)
        for a in range(4):
            b = a ^ 1
            (cp, cp, act, act)[a](["Q2"], ["Q3%d" % a], qq(Q3, 0, 16, 1, 32 * a, 32), qq(Q2, 0, 16, 1, 32 * b, 32))
        tt(["Q2", "Q30", "Q31", "Q32", "Q33", "Q4z"], ["Q4"], qq(Q4, 0, 16), qq(Q2, 0, 16), qq(Q3, 0, 16), OP.add)
        turn(["Q4", "Q4z"], ["Q5"], qq(Q5), qq(Q4))
        tt(["Q5"], ["Q6"], qq(Q6, 0, 16), qq(Q5, 0, 16), qq(Q5, 16, 32), OP.add)
        tt(["Q5"], ["Q6b"], qq(Q6, 16, 32), qq(Q5, 0, 16), qq(Q5, 16, 32), OP.add)
        turn(["Q6", "Q6b"], ["Q7"], qq(Q7), qq(Q6))
        send_columns()
        act(["Q7", "OU2"], ["RP"], T.RP[:], qq(Q7).indirect(BC32))
        turn(["RP"], ["TO"], T.TO[:], T.RP[:])
        act(["TO", "qn"], ["AJ0", "AC"], T.AJ[:, 0:256], T.TO[:], AF.Sign, T.PF[:, 4:5], 1.0, T.SC[:, 0:1])
        ts(["AC"], ["F1"], T.SC[:, 2:3], T.SC[:, 0:1], 64.0, OP.is_le)
        ts(["ON", "F1"], ["FB"], T.FB[:, 0:32], T.ON[:, 0:32], T.SC[:, 2:3], OP.mult, -15.5 / 16, OP.add)
        turn(["FB"], ["FX"], T.FB[:, 64:96], T.FB[:, 0:32])
        emit("V", ["FX"], ["SF"], lambda e: e.tensor_reduce(T.SC[:, 4:5], T.FB[:, 64:80], AxisListType.X, OP.add))
        act(["TO", "SF"], ["AJ1", "NP"], T.AJ[:, 256:512], T.TO[:], AF.Sign, T.SC[:, 4:5], 1.0, T.SC[:, 5:6])
        ts(["TO", "SF"], ["EQM"], T.EQM[:], T.TO[:], T.SC[:, 4:5], OP.add, 0.5, OP.is_equal)
        scan(["EQM", "ZR"], ["CU"], T.CU[:], T.EQM[:], T.ON[:, 32:288], 32.0, OP.add, OP.max)
        ts(["CU", "NP"], ["OV"], T.OV[:], T.CU[:], 2.0, OP.mult, T.SC[:, 5:6], OP.is_gt)
        tt(["TO", "OV"], ["Zx"], T.Z2[:], T.TO[:], T.OV[:], OP.add)
        ts(["Zx", "SF"], ["GN"], T.GN[:], T.Z2[:], T.SC[:, 4:5], OP.add, 0.5, OP.is_le)
        scan(["GN", "ZR"], ["GS"], T.GS[:], T.GN[:], T.ON[:, 32:288], 255.0, OP.add, OP.max)
        scan(["GS", "GN"], ["M1"], T.M1[:], T.GS[:], T.GN[:], 0.0, OP.max, OP.mult)
        tt(["M1", "ID"], ["Y0"], T.Y0[:], T.M1[:], T.ID[:], OP.max)
        scan(["EX", "M1"], ["NSx"], T.NS[:], T.EX[:], T.M1[:], 0.0, OP.add, OP.max)
        tt(["NSx", "CP"], ["NSw"], T.W3[:, 0:16], T.NS[:, E15], T.W3[:, 16:32], OP.max)
        ts(["NSw", "xq"], ["NI16"], T.NI16[:], T.W3[:, 0:16], T.PF[:, 5:6], OP.subtract)
        act(["NSw", "nxq"], ["NS"], T.CL[:, 32:48], T.W3[:, 0:16], AF.Identity, T.PF[:, 14:15])
        for b in range(4):
            k = PS[b]
            mm(["L%d" % t, "pad", "W"], k, 128, "W", 128 * b, "L", lo, True, False)
            mm(["L%d" % t, "pad", "KR%d" % b], k, 128, "KR%d" % b, 0, "L", lo, False, True)
        for b in range(2):
            act([PS[b], "RTz"], ["RT%d" % b], T.RT[:, b:384:4], T[PS[b]][:, 0:96], AF.Copy, 0.0, 2.0 ** -7)
        for b in range(2, 4):
            ts([PS[b], "RTz"], ["RT%d" % b], T.RT[:, b:384:4], T[PS[b]][:, 0:96], 2.0 ** -7, OP.mult)
        quant(["RT0", "RT1", "RT2", "RT3", "RTz"], "P", 256, 384, T.RT[:])
        XN = "X%d" % (t + 1)
        emit("V", ["P", "Pb", "NI16"], [XN], lambda e, t=t: e.tensor_copy(
            T.cX[:, 256 * t + 256:256 * t + 512].bitcast(dt.uint32), T.cP[:, :].bitcast(dt.uint32).indirect(T.NI16[:])))
        emit("A", ["P", "Pb", "NI16"], [XN + "s"], lambda e, t=t: e.activation(
            T.sX[:, 256 * t + 256:256 * t + 512], T.sP[:, :].indirect(T.NI16[:]), AF.Copy))
        act(["NSw", "nxq"], ["NS2"], T.CL[:, 48:64], T.W3[:, 0:16], AF.Identity, T.PF[:, 14:15])
        ts(["NS", "NS2"], ["GW"], T.SM[:, 0:32], T.CL[:, 32:64], 256.0, OP.is_ge)
        tt(["NS", "LW", "CL"], ["D1"], T.SM[:, 32:64], T.CL[:, 16:48], T.CL[:, 0:32], OP.subtract)
        tt(["GW", "D1"], ["D2"], T.SM[:, 64:96], T.SM[:, 0:32], T.SM[:, 32:64], OP.mult)
        tt(["D2", "LW", "CL"], ["D3"], T.SM[:, 96:128], T.SM[:, 64:96], T.CL[:, 0:32], OP.add)
        cp(["D3"], ["M16"], T.M16[:], T.SM[:, 96:128])

        def chain(t=t):
            src, k = T.Y0, "Y0"
            for i in range(5):
                dst, kd = ((T.YA, "YA"), (T.YB, "YB"))[i % 2] if i < 4 else (T.YX, "YX")
                act([k, "M16"], [kd], dst[:, 0:256], src[:, 0:256].indirect(T.M16[:, 0:16]))
                src, k = dst, kd
            act(["YX", "YXe", "M16"], ["M1"], T.M1[:], T.YX[:].indirect(T.M16[:, 16:32]))

        def unpack(t=t):
            LL = "LL%d" % t
            cp([LL], ["LI0"], T.LI[:, 0:48], T.LL[:, 48 * t:48 * t + 48])
            ts(["LI0"], ["LI1"], T.LI[:, 48:96], T.LI[:, 0:48], 255, OP.bitwise_and)
            ts(["LI0"], ["LI2"], T.LI[:, 96:144], T.LI[:, 0:48], 8, OP.arith_shift_right)
            cp(["LI1", "LI2"], ["YXe"], T.YX[:, 256:352], T.LI[:, 48:144])

        def relink():
            scan(["EX", "M1"], ["NRx"], T.NR[:], T.EX[:], T.M1[:], 0.0, OP.add, OP.max)
            r = T.SM[:, 144:160]
            sm = [T.SM[:, 160 + 16 * i:176 + 16 * i] for i in range(3)]
            act(["NRx", "nxq"], ["NR"], r, T.NR[:, E15], AF.Identity, T.PF[:, 14:15])
            ts(["NR"], ["FL"], sm[0], r, 256.0, OP.is_ge)
            tt(["CW", "NR"], ["G1"], sm[1], T.CW[:], r, OP.subtract)
            tt(["FL", "G1"], ["G2"], sm[2], sm[0], sm[1], OP.mult)
            tt(["G2", "NR"], ["LW"], T.CL[:, 16:32], sm[2], r, OP.add)
            cp(["LW"], ["L16"], T.L16[:], T.CL[:, 16:32])
        pending = [unpack, chain, relink]

    mm(["V", "X3", "X3s"], "P7", 256, "V", 0, "X3", 0)
    dma("S", "dOc", ["X3", "X3s"], ["oc"], [(T.oc[:, :], T.cX[:, 768:1024].bitcast(dt.uint8))] + [
        (T.osc[4 * k:4 * k + 4, :], T.sX[32 * k:32 * k + 4, 768:1024]) for k in range(4)])
    pending[0]()
    pending[1]()
    cp(["P7"], ["YO"], T.YO[:], T.P7[:, 0:256])
    dma("S", "dY", ["YO"], ["y"], [(T.y[:, :], T.YO[:])])
    ts(["M1"], ["GS"], T.GS[:], T.M1[:], 256.0, OP.is_ge)
    tt(["ID", "M1"], ["NRx"], T.NR[:], T.ID[:], T.M1[:], OP.subtract)
    tt(["GS", "NRx"], ["Y0"], T.Y0[:], T.GS[:], T.NR[:], OP.mult)
    tt(["Y0", "M1"], ["NSx", "NS"], T.NS[:], T.Y0[:], T.M1[:], OP.add)
    dma("S", "dLk", ["NS"], ["lk"], [(T.lk[:, :], T.NS[0:128:16, :])])
    schedule()
    for s in cnt:
        if known["S"].get(s, 0) < cnt[s]:
            g.sync.wait_ge(T.sem[s], cnt[s])
    g.wait_ge(T.sem.ls, sent[0])
